import numpy as np
import ml_dtypes


def mxq(x, axis, fmt="e4m3"):
    dtype, down = {"e4m3": (ml_dtypes.float8_e4m3fn, 7), "e5m2": (ml_dtypes.float8_e5m2, 14)}[fmt]
    v = np.moveaxis(np.asarray(x, np.float32).astype(ml_dtypes.bfloat16).astype(np.float64), axis, -1)
    blocks = v.reshape(v.shape[:-1] + (-1, 32))
    amax = np.abs(blocks).max(-1, keepdims=True)
    byte = np.maximum(np.where(amax > 0, np.frexp(amax)[1] - 1 + 127, 0) - down, 1)
    scale = np.exp2(byte - 127.0)
    codes = (blocks / scale).astype(np.float32).astype(dtype).astype(np.float64)
    return np.moveaxis((codes * scale).reshape(v.shape), -1, axis)


WIDE = False


def mx_kscale(k):
    if not WIDE:
        return np.ones(k)
    levels = np.array([10, -10, 5, -5, 0])
    if k % 512:
        return np.exp2(np.random.permutation(np.resize(levels, k // 32))).repeat(32)
    a = np.empty((k // 512, 16))
    for p in range(k // 512):
        a[p, :8] = np.random.permutation(np.resize(levels, 8))
        for g in range(8):
            far = levels[np.abs(levels - a[p, g]) >= 10]
            a[p, g + 8] = far[np.random.randint(len(far))]
    return np.exp2(a.ravel()).repeat(32)


BF16 = ml_dtypes.bfloat16


def bf(x):
    return np.asarray(x, np.float32).astype(BF16)


def f64(x):
    return np.asarray(x).astype(np.float64)


B, D, F, K = 4096, 512, 512, 2


def draw0():
    u, t = mx_kscale(D), mx_kscale(F)
    return {
        "x": bf(np.random.standard_normal((B, D)) * u),
        "cs": bf(np.random.standard_normal((K, D, F)) / np.sqrt(D) / u[None, :, None]),
        "ss": bf(np.random.standard_normal((K, D, F)) / np.sqrt(D) / u[None, :, None]),
        "gamma": bf(np.random.uniform(0.5, 1.5, (K, F))),
        "g": bf((1.0 + 0.1 * np.random.standard_normal(F)) * t),
        "dv": bf(np.random.standard_normal((F, D)) / np.sqrt(F) / t[:, None]),
    }


def weno_alpha(s, gamma_k):
    d = 0.5 + s * s
    return gamma_k / (d * d)


def burgers_flux(qh):
    return qh + 0.5 * qh * qh


def core(x, cs, ss, gamma, g, dv):
    cs, ss, gamma, g = f64(cs), f64(ss), f64(gamma), f64(g)
    xq = mxq(f64(x), 1, "e4m3")
    q = [(xq @ mxq(cs[k], 0, "e4m3")) for k in range(K)]
    s = [(xq @ mxq(ss[k], 0, "e4m3")) for k in range(K)]
    al = [weno_alpha(s[k], gamma[k][None, :]) for k in range(K)]
    qh = (al[0] * q[0] + al[1] * q[1]) / (al[0] + al[1])
    phi = burgers_flux(qh)
    pg = phi * g[None, :]
    return mxq(pg, 1, "e4m3") @ mxq(f64(dv), 0, "e4m3")


def e4m3fn_bytes(y):
    return np.clip(np.asarray(y, np.float64), -448.0, 448.0).astype(np.float32).astype(ml_dtypes.float8_e4m3fn).view(np.uint8)


def e4m3fn_values(b):
    return np.asarray(b, np.uint8).view(ml_dtypes.float8_e4m3fn).astype(np.float64)


def setup_inputs():
    d = draw0()
    x0 = np.asarray(d['x']).astype(np.float64)
    s = (np.max(np.abs(x0), axis=(0,), keepdims=True) / 448.0).astype(np.float32)
    out = {}
    for k, v in d.items():
        if k == 'x':
            out['x_bytes'] = e4m3fn_bytes(x0 / s.astype(np.float64))
            out['x_scale'] = s
        else:
            out[k] = v
    return out


def reference(x_bytes, x_scale, cs, ss, gamma, g, dv):
    return core(e4m3fn_values(x_bytes) * x_scale.astype(np.float64), cs, ss, gamma, g, dv)

@@ -1,0 +1,413 @@
+from contextlib import ExitStack
+
+import concourse.mybir as mybir
+from concourse.masks import make_identity
+
+B, D, F = 4096, 512, 512
+FLOPS = 5 * 2 * B * D * F
+
+P = 128
+TOK = 512
+TILES = B // TOK
+SUB = TOK // P
+
+F32 = mybir.dt.float32
+BF16 = mybir.dt.bfloat16
+U32 = mybir.dt.uint32
+U8 = mybir.dt.uint8
+FP8 = mybir.dt.float8_e4m3fn
+FP8X4 = mybir.dt.float8_e4m3fn_x4
+ALU = mybir.AluOpType
+ACT = mybir.ActivationFunctionType
+
+E_ON_V = (0, 2, 3, 4, 5, 6, 7)
+V_ON_S = (4,)
+GSIZE = (4, 3, 1)
+QS = (0, 5, 17)
+QN = (0, 8, 9)
+XA = 2
+ZL = 3
+FL = 3
+
+
+def tile_learnedstencilwenostep_t_kernel(tc, x_bytes, x_scale, cs, ss, gamma, g, dv, out):
+    nc = tc.nc
+    with ExitStack() as ctx:
+        keep = ctx.enter_context(tc.tile_pool(name="keep", bufs=1))
+        wst = ctx.enter_context(tc.tile_pool(name="wst", bufs=2))
+        st = ctx.enter_context(tc.tile_pool(name="st", bufs=2))
+        psum = ctx.enter_context(tc.psum_pool(name="psum", bufs=1))
+        ctx.enter_context(tc.manual_schedule())
+
+        scale = keep.tile([P, D], F32, name="scale")
+        xby = {}
+
+        def load_x(i):
+            t = st.tile([P, SUB, D], U8, name="xby", bufs=4)
+            rows = x_bytes[i * TOK : (i + 1) * TOK, :]
+            nc.sync.dma_start(out=t[:], in_=rows.rearrange("(p b) k -> p b k", b=SUB))
+            xby[i] = t
+
+        wraw = {}
+
+        def load_w(name, src, eng):
+            t = wst.tile([P, 4, 512], BF16, name="wraw", bufs=3)
+            eng.dma_start(out=t[:], in_=src.rearrange("(p j) c -> p j c", j=4))
+            wraw[name] = t
+
+        gam = keep.tile([P, 2, 4], BF16, name="gam")
+        gcol = keep.tile([P, 4], BF16, name="gcol")
+        load_x(0)
+        nc.scalar.dma_start(out=scale[:], in_=x_scale.rearrange("o k -> (o k)").partition_broadcast(P))
+        load_w("s0", ss[0], nc.sync)
+        load_w("s1", ss[1], nc.sync)
+        nc.scalar.dma_start(out=gam[:], in_=gamma.rearrange("k (p t) -> p k t", t=4))
+        nc.scalar.dma_start(out=gcol[:], in_=g.rearrange("(p t) -> p t", t=4))
+        load_x(1)
+        load_w("c1", cs[1], nc.sync)
+
+        ident = keep.tile([P, P], F32, name="ident")
+        make_identity(nc, ident[:])
+        half = keep.tile([P, 1], F32, name="half")
+        nc.vector.memset(half[:], 0.5)
+
+        lgam = keep.tile([P, 2, 4], F32, name="lgam")
+        lrho = keep.tile([P, 4], F32, name="lrho")
+        gfull = keep.tile([P, 4], F32, name="gfull")
+        ghalf = keep.tile([P, 4], F32, name="ghalf")
+
+        def constants_s():
+            nc.scalar.activation(out=lgam[:], in_=gam[:], func=ACT.Ln)
+
+        def constants_v():
+            nc.vector.tensor_tensor(out=lrho[:], in0=lgam[:, 1, :], in1=lgam[:, 0, :], op=ALU.subtract)
+            nc.vector.tensor_copy(out=gfull[:], in_=gcol[:])
+            nc.vector.tensor_scalar(out=ghalf[:], in0=gcol[:], scalar1=0.5, scalar2=None, op0=ALU.mult)
+
+        wgrp = {}
+        codes = {}
+        scales = {}
+
+        def w_group(name, raw, eng, sign=1.0, permute=True):
+            grp = wst.tile([P, 2048], BF16, name="wgrp", bufs=3, align_bytes=64)
+            if permute:
+                o = grp[:].rearrange("p (t m j) -> p t m j", t=4, j=4)
+                i = raw[:].rearrange("p j (m t) -> p t m j", t=4)
+            else:
+                o = grp[:].rearrange("p (c j) -> p c j", j=4)
+                i = raw[:].rearrange("p j c -> p c j")
+            if eng == "v":
+                if sign == 1.0:
+                    nc.vector.tensor_copy(out=o, in_=i)
+                else:
+                    nc.vector.tensor_scalar(out=o, in0=i, scalar1=sign, scalar2=None, op0=ALU.mult)
+            elif eng == "s":
+                if sign == 1.0:
+                    nc.scalar.copy(out=o, in_=i)
+                else:
+                    nc.scalar.activation(out=o, in_=i, func=ACT.Copy, scale=sign)
+            wgrp[name] = grp
+
+        def w_quant(name):
+            codes[name] = keep.tile([P, 512], U32, name="codes_" + name, align_bytes=64)
+            scales[name] = keep.tile([P, 512], U8, name="scales_" + name, align_bytes=64)
+            nc.vector.quantize_mx(out=codes[name][:].bitcast(FP8X4), scales=scales[name][:], in_=wgrp[name][:])
+
+        xw = {}
+        xps = {}
+        xg = {}
+        xc = {}
+        xs = {}
+
+        def widen(i):
+            t = st.tile([P, SUB * D], BF16, name="xw", bufs=2)
+            for b in range(SUB):
+                nc.vector.tensor_tensor(out=t[:, b * D : (b + 1) * D], in0=xby[i][:, b, :].bitcast(FP8), in1=scale[:], op=ALU.mult)
+            xw[i] = t
+
+        def turn(i, h):
+            ps = psum.tile([P, 2, 2, P], F32, name="xps", bufs=1)
+            for b in range(2):
+                c0 = (2 * h + b) * D
+                words = xw[i][:, c0 : c0 + D].bitcast(F32)
+                for u in range(2):
+                    nc.tensor.transpose(ps[:, b, u, :], words[:, u : D // 2 : 2], ident[:])
+            xps[i, h] = ps
+
+        def empty_x(i, h):
+            if h == 0:
+                xg[i] = st.tile([P, TOK * 4], BF16, name="xg", bufs=2, align_bytes=64)
+            o = xg[i][:, h * 1024 : (h + 1) * 1024].bitcast(F32).rearrange("p (b n u) -> p b n u", b=2, u=2)
+            src = xps[i, h][:].rearrange("p b u n -> p b n u")
+            if i in E_ON_V:
+                nc.vector.tensor_copy(out=o, in_=src)
+            else:
+                nc.scalar.copy(out=o, in_=src)
+
+        def quant_x(i):
+            xc[i] = st.tile([P, TOK], U32, name="xc", bufs=TILES, align_bytes=64)
+            xs[i] = st.tile([P, TOK], U8, name="xs", bufs=TILES, align_bytes=64)
+            nc.vector.quantize_mx(out=xc[i][:].bitcast(FP8X4), scales=xs[i][:], in_=xg[i][:])
+
+        def mm(ps, w, t, i, start, stop):
+            nc.tensor.matmul_mx(
+                out=ps[:],
+                lhsT=codes[w][:, t * P : (t + 1) * P].bitcast(FP8X4),
+                lhsT_scale=scales[w][:, t * P : (t + 1) * P],
+                rhs=xc[i][:].bitcast(FP8X4),
+                rhs_scale=xs[i][:],
+                start=start,
+                stop=stop,
+            )
+
+        a = {}
+
+        def square(i, k, t):
+            if t == 0:
+                a[i, k] = st.tile([P, 4 * TOK], F32, name="a%d" % k, bufs=7 if k == 0 else 2)
+            ps = psum.tile([P, TOK], F32, name="sps", tag="sps", bufs=3)
+            mm(ps, "s%d" % k, t, i, True, True)
+            nc.scalar.activation(out=a[i, k][:, t * TOK : (t + 1) * TOK], in_=ps[:], func=ACT.Square)
+
+        def log(i, k):
+            nc.scalar.activation(out=a[i, k][:], in_=a[i, k][:], func=ACT.Ln, bias=half[:, 0:1])
+
+        def zsub(i):
+            nc.vector.tensor_tensor(out=a[i, 0][:], in0=a[i, 0][:], in1=a[i, 1][:], op=ALU.subtract)
+
+        def sigmoid(i):
+            for t in range(4):
+                z = a[i, 0][:, t * TOK : (t + 1) * TOK]
+                nc.scalar.activation(out=z, in_=z, func=ACT.Sigmoid, bias=lrho[:, t : t + 1], scale=2.0)
+
+        qh = {}
+        dps = {}
+        qps = {}
+        vv = {}
+        pg = {}
+        pc = {}
+        psc = {}
+
+        def cand(i, t):
+            dps[i, t] = psum.tile([P, TOK], F32, name="dps", bufs=2)
+            mm(dps[i, t], "c1", t, i, True, False)
+            mm(dps[i, t], "n0", t, i, False, True)
+            qps[i, t] = psum.tile([P, TOK], F32, name="qps", bufs=2)
+            mm(qps[i, t], "c0", t, i, True, True)
+
+        def blend_m(i, t):
+            if t == 0:
+                qh[i] = st.tile([P, 4 * TOK], F32, name="qh", bufs=2)
+            s_ = slice(t * TOK, (t + 1) * TOK)
+            nc.vector.tensor_tensor(out=qh[i][:, s_], in0=a[i, 0][:, s_], in1=dps[i, t][:], op=ALU.mult)
+
+        def blend_q(i, t):
+            s_ = slice(t * TOK, (t + 1) * TOK)
+            nc.vector.tensor_tensor(out=qh[i][:, s_], in0=qh[i][:, s_], in1=qps[i, t][:], op=ALU.add)
+
+        def vgain(i, t):
+            if t == 0:
+                vv[i] = st.tile([P, 4 * TOK], F32, name="vv", bufs=2)
+            s_ = slice(t * TOK, (t + 1) * TOK)
+            if i in V_ON_S:
+                nc.scalar.activation(out=vv[i][:, s_], in_=qh[i][:, s_], func=ACT.Identity, scale=ghalf[:, t : t + 1], bias=gfull[:, t : t + 1])
+            else:
+                nc.vector.tensor_scalar(out=vv[i][:, s_], in0=qh[i][:, s_], scalar1=ghalf[:, t : t + 1], scalar2=gfull[:, t : t + 1], op0=ALU.mult, op1=ALU.add)
+
+        def flux(i):
+            pg[i] = st.tile([P, TOK * 4], BF16, name="pg", bufs=2, align_bytes=64)
+            o = pg[i][:].rearrange("p (c i t) -> p c t i", i=2, t=4)
+            q_ = qh[i][:].rearrange("p (t c i) -> p c t i", t=4, i=2)
+            v_ = vv[i][:].rearrange("p (t c i) -> p c t i", t=4, i=2)
+            nc.vector.tensor_tensor(out=o, in0=q_, in1=v_, op=ALU.mult)
+
+        def quant_p(i):
+            pc[i] = st.tile([P, TOK], U32, name="pc", bufs=2, align_bytes=64)
+            psc[i] = st.tile([P, TOK], U8, name="psc", bufs=2, align_bytes=64)
+            nc.vector.quantize_mx(out=pc[i][:].bitcast(FP8X4), scales=psc[i][:], in_=pg[i][:])
+
+        osb = {}
+
+        def div(i, b):
+            if b == 0:
+                osb[i] = st.tile([P, SUB, D], F32, name="osb", bufs=2)
+            ps = psum.tile([P, D], F32, name="ops", tag="sps", bufs=3)
+            nc.tensor.matmul_mx(
+                out=ps[:],
+                lhsT=pc[i][:, b * P : (b + 1) * P].bitcast(FP8X4),
+                lhsT_scale=psc[i][:, b * P : (b + 1) * P],
+                rhs=codes["dv"][:].bitcast(FP8X4),
+                rhs_scale=scales["dv"][:],
+                start=True,
+                stop=True,
+            )
+            nc.scalar.copy(out=osb[i][:, b, :], in_=ps[:])
+            rows = out[i * TOK : (i + 1) * TOK, :].rearrange("(p b) d -> p b d", b=SUB)
+            if i == TILES - 1:
+                nc.sync.dma_start(out=rows[:, b, :], in_=osb[i][:, b, :])
+            elif b == SUB - 1:
+                nc.sync.dma_start(out=rows, in_=osb[i][:])
+
+        from_slot = {}
+
+        def at(slot, fn, *args):
+            from_slot.setdefault(slot, []).append((fn, args))
+
+        def logh(i, k, h):
+            z = a[i, k][:, h * 1024 : (h + 1) * 1024]
+            nc.scalar.activation(out=z, in_=z, func=ACT.Ln, bias=half[:, 0:1])
+
+        def zsubh(i, h):
+            s_ = slice(h * 1024, (h + 1) * 1024)
+            nc.vector.tensor_tensor(out=a[i, 0][:, s_], in0=a[i, 0][:, s_], in1=a[i, 1][:, s_], op=ALU.subtract)
+
+        def widen_b(i, b):
+            if b == 0:
+                xw[i] = st.tile([P, SUB * D], BF16, name="xw", bufs=2)
+            nc.vector.tensor_tensor(out=xw[i][:, b * D : (b + 1) * D], in0=xby[i][:, b, :].bitcast(FP8), in1=scale[:], op=ALU.mult)
+
+        def turn_b(i, b):
+            h = b // 2
+            if b % 2 == 0:
+                xps[i, h] = psum.tile([P, 2, 2, P], F32, name="xps", bufs=1)
+            words = xw[i][:, b * D : (b + 1) * D].bitcast(F32)
+            for u in range(2):
+                nc.tensor.transpose(xps[i, h][:, b % 2, u, :], words[:, u : D // 2 : 2], ident[:])
+
+        def flux_h(i, h):
+            if h == 0:
+                pg[i] = st.tile([P, TOK * 4], BF16, name="pg", bufs=2, align_bytes=64)
+            o = pg[i][:, h * 1024 : (h + 1) * 1024].rearrange("p (c i t) -> p c t i", i=2, t=4)
+            q_ = qh[i][:].rearrange("p (t h c i) -> p h c t i", t=4, i=2, h=2)[:, h]
+            v_ = vv[i][:].rearrange("p (t h c i) -> p h c t i", t=4, i=2, h=2)[:, h]
+            nc.vector.tensor_tensor(out=o, in0=q_, in1=v_, op=ALU.mult)
+
+        def quant_ph(i, h):
+            if h == 0:
+                pc[i] = st.tile([P, TOK], U32, name="pc", bufs=2, align_bytes=64)
+                psc[i] = st.tile([P, TOK], U8, name="psc", bufs=2, align_bytes=64)
+            s_ = slice(h * 256, (h + 1) * 256)
+            nc.vector.quantize_mx(out=pc[i][:, s_].bitcast(FP8X4), scales=psc[i][:, s_], in_=pg[i][:, h * 1024 : (h + 1) * 1024])
+
+        pq = []
+        tq = []
+
+        def run_due(queue, now, all_=False):
+            rest = []
+            for due, fn, args in queue:
+                if due <= now or all_:
+                    fn(*args)
+                else:
+                    rest.append((due, fn, args))
+            queue[:] = rest
+
+        def p_slot(p):
+            i, t = p // 4, p % 4
+            square(i, 0, t)
+            square(i, 1, t)
+            run_due(pq, p)
+            if i + XA < TILES:
+                widen_b(i + XA, t)
+                pq.append((p + 1, turn_b, (i + XA, t)))
+                if t == 1:
+                    pq.append((p + 2, empty_x, (i + XA, 0)))
+                if t == 3:
+                    pq.append((p + 2, empty_x, (i + XA, 1)))
+                    pq.append((p + 3, quant_x, (i + XA,)))
+            if t % 2 == 1:
+                h = t // 2
+                pq.append((p + 1, logh, (i, 0, h)))
+                pq.append((p + 1, logh, (i, 1, h)))
+                pq.append((p + ZL, zsubh, (i, h)))
+            if t == 3 and i + 4 < TILES:
+                load_x(i + 4)
+
+        def t_slot(q):
+            l, t = q // 4, q % 4
+            if q == 0:
+                cand(0, 0)
+            if q + 1 < navail:
+                cand((q + 1) // 4, (q + 1) % 4)
+            elif q + 1 < 4 * TILES:
+                tq.append((q + 1, cand, ((q + 1) // 4, (q + 1) % 4)))
+            blend_m(l, t)
+            run_due(tq, q)
+            blend_q(l, t)
+            tq.append((q + 1, vgain, (l, t)))
+            if t == 3:
+                f = q + (FL if l in V_ON_S else 1)
+                tq.append((f, flux_h, (l, 0)))
+                tq.append((f + 1, flux_h, (l, 1)))
+                tq.append((f + 1, quant_ph, (l, 0)))
+                tq.append((f + 2, quant_ph, (l, 1)))
+                for b in range(SUB):
+                    tq.append((f + 2 + b, div, (l, b)))
+
+        def wprep(name, raw, eng, **kw):
+            w_group(name, wraw[raw], eng, **kw)
+
+        dummy = keep.tile([P, 1], F32, name="dummy")
+        nc.scalar.activation(out=dummy[:], in_=half[:], func=ACT.Ln)
+        wprep("s1", "s1", "s")
+        for b in range(SUB):
+            widen_b(0, b)
+            turn_b(0, b)
+            if b == 1:
+                wprep("s0", "s0", "v")
+        empty_x(0, 0)
+        w_quant("s0")
+        empty_x(0, 1)
+        quant_x(0)
+        w_quant("s1")
+        constants_s()
+        constants_v()
+        load_w("c0", cs[0], nc.sync)
+        load_x(2)
+        load_w("dv", dv, nc.sync)
+        load_x(3)
+        for x in range(1, XA):
+            for b in range(SUB):
+                widen_b(x, b)
+                turn_b(x, b)
+                if b == 2:
+                    empty_x(x, 0)
+            empty_x(x, 1)
+            quant_x(x)
+        WORK = {
+            2: [(wprep, ("c1", "c1", "v"), {}), ],
+            4: [(w_quant, ("c1",), {})],
+            5: [(wprep, ("c0", "c0", "v"), {})],
+            7: [(w_quant, ("c0",), {})],
+            8: [(wprep, ("n0", "c0", "v"), {"sign": -1.0})],
+            10: [(w_quant, ("n0",), {})],
+            11: [(wprep, ("dv", "dv", "v"), {"permute": False})],
+            13: [(w_quant, ("dv",), {})],
+        }
+        q = 0
+        navail = 0
+        p = 0
+        for gi, n in enumerate(GSIZE):
+            for s in range(4 * n):
+                p_slot(p)
+                for fn, ar, kw in WORK.get(p, []):
+                    fn(*ar, **kw)
+                p += 1
+                if gi > 0:
+                    target = QS[gi] + (s + 1) * QN[gi] // (4 * n)
+                    while q < min(target, 4 * (p // 4 - 0) ) and q < navail:
+                        t_slot(q)
+                        q += 1
+            run_due(pq, 0, True)
+            first = p // 4 - n
+            for i in range(first, first + n):
+                sigmoid(i)
+            navail = 4 * (first + n)
+            if gi + 1 < len(GSIZE):
+                while q < QS[gi + 1]:
+                    t_slot(q)
+                    q += 1
+        while q < 4 * TILES:
+            t_slot(q)
+            q += 1
+        for s in range(12):
+            run_due(tq, q + s)

@@ -20,14 +20,16 @@ FP8X4 = mybir.dt.float8_e4m3fn_x4
 ALU = mybir.AluOpType
 ACT = mybir.ActivationFunctionType
 
-E_ON_V = (0, 2, 3, 4, 5, 6, 7)
-V_ON_S = (4,)
-GSIZE = (4, 3, 1)
-QS = (0, 5, 17)
-QN = (0, 8, 9)
-XA = 2
-ZL = 3
-FL = 3
+E_ON_V = range(1, 8)
+PROGRAM = ((0,None,(),2),(1,None,(),2),(2,None,(),2),(None,None,(0,1,2),2),(3,0),(4,1),(5,None),(None,2,(3,4,5)),(6,3),(7,4),(None,5,(6,7)),(None,6),(None,7))
+VG = (2,2,2,2,2,2,2,2)
+VG3 = ()
+ZPOS = 0
+Z_ON_G = ()
+WE = 'vvnv'
+WN = 2
+XB = 1
+O_ON_V = ()
 
 
 def tile_learnedstencilwenostep_t_kernel(tc, x_bytes, x_scale, cs, ss, gamma, g, dv, out):
@@ -37,9 +39,9 @@ def tile_learnedstencilwenostep_t_kernel(tc, x_bytes, x_scale, cs, ss, gamma, g,
         wst = ctx.enter_context(tc.tile_pool(name="wst", bufs=2))
         st = ctx.enter_context(tc.tile_pool(name="st", bufs=2))
         psum = ctx.enter_context(tc.psum_pool(name="psum", bufs=1))
-        ctx.enter_context(tc.manual_schedule())
+        ctx.enter_context(tc.manual_schedule(engines={mybir.EngineType.Activation}))
 
-        scale = keep.tile([P, D], F32, name="scale")
+        scale = keep.tile([P, 2 * D], F32, name="scale")
         xby = {}
 
         def load_x(i):
@@ -58,9 +60,9 @@ def tile_learnedstencilwenostep_t_kernel(tc, x_bytes, x_scale, cs, ss, gamma, g,
         gam = keep.tile([P, 2, 4], BF16, name="gam")
         gcol = keep.tile([P, 4], BF16, name="gcol")
         load_x(0)
-        nc.scalar.dma_start(out=scale[:], in_=x_scale.rearrange("o k -> (o k)").partition_broadcast(P))
-        load_w("s0", ss[0], nc.sync)
+        nc.scalar.dma_start(out=scale[:, :D], in_=x_scale.rearrange("o k -> (o k)").partition_broadcast(P))
         load_w("s1", ss[1], nc.sync)
+        load_w("s0", ss[0], nc.sync)
         nc.scalar.dma_start(out=gam[:], in_=gamma.rearrange("k (p t) -> p k t", t=4))
         nc.scalar.dma_start(out=gcol[:], in_=g.rearrange("(p t) -> p t", t=4))
         load_x(1)
@@ -101,6 +103,10 @@ def tile_learnedstencilwenostep_t_kernel(tc, x_bytes, x_scale, cs, ss, gamma, g,
                     nc.vector.tensor_copy(out=o, in_=i)
                 else:
                     nc.vector.tensor_scalar(out=o, in0=i, scalar1=sign, scalar2=None, op0=ALU.mult)
+            elif eng == "n":
+                nc.vector.tensor_scalar(out=grp[:], in0=wgrp["c0"][:], scalar1=-1.0, scalar2=None, op0=ALU.mult)
+            elif eng == "g":
+                nc.gpsimd.tensor_scalar(out=o, in0=i, scalar1=sign, scalar2=0.0, op0=ALU.mult, op1=ALU.add)
             elif eng == "s":
                 if sign == 1.0:
                     nc.scalar.copy(out=o, in_=i)
@@ -205,15 +211,6 @@ def tile_learnedstencilwenostep_t_kernel(tc, x_bytes, x_scale, cs, ss, gamma, g,
             s_ = slice(t * TOK, (t + 1) * TOK)
             nc.vector.tensor_tensor(out=qh[i][:, s_], in0=qh[i][:, s_], in1=qps[i, t][:], op=ALU.add)
 
-        def vgain(i, t):
-            if t == 0:
-                vv[i] = st.tile([P, 4 * TOK], F32, name="vv", bufs=2)
-            s_ = slice(t * TOK, (t + 1) * TOK)
-            if i in V_ON_S:
-                nc.scalar.activation(out=vv[i][:, s_], in_=qh[i][:, s_], func=ACT.Identity, scale=ghalf[:, t : t + 1], bias=gfull[:, t : t + 1])
-            else:
-                nc.vector.tensor_scalar(out=vv[i][:, s_], in0=qh[i][:, s_], scalar1=ghalf[:, t : t + 1], scalar2=gfull[:, t : t + 1], op0=ALU.mult, op1=ALU.add)
-
         def flux(i):
             pg[i] = st.tile([P, TOK * 4], BF16, name="pg", bufs=2, align_bytes=64)
             o = pg[i][:].rearrange("p (c i t) -> p c t i", i=2, t=4)
@@ -241,38 +238,53 @@ def tile_learnedstencilwenostep_t_kernel(tc, x_bytes, x_scale, cs, ss, gamma, g,
                 start=True,
                 stop=True,
             )
-            nc.scalar.copy(out=osb[i][:, b, :], in_=ps[:])
+            if (i, b) in O_ON_V:
+                nc.vector.tensor_copy(out=osb[i][:, b, :], in_=ps[:])
+            else:
+                nc.scalar.copy(out=osb[i][:, b, :], in_=ps[:])
             rows = out[i * TOK : (i + 1) * TOK, :].rearrange("(p b) d -> p b d", b=SUB)
             if i == TILES - 1:
                 nc.sync.dma_start(out=rows[:, b, :], in_=osb[i][:, b, :])
             elif b == SUB - 1:
                 nc.sync.dma_start(out=rows, in_=osb[i][:])
 
-        from_slot = {}
-
-        def at(slot, fn, *args):
-            from_slot.setdefault(slot, []).append((fn, args))
-
-        def logh(i, k, h):
-            z = a[i, k][:, h * 1024 : (h + 1) * 1024]
+        def logk(i, k):
+            z = a[i, k][:]
             nc.scalar.activation(out=z, in_=z, func=ACT.Ln, bias=half[:, 0:1])
 
-        def zsubh(i, h):
-            s_ = slice(h * 1024, (h + 1) * 1024)
-            nc.vector.tensor_tensor(out=a[i, 0][:, s_], in0=a[i, 0][:, s_], in1=a[i, 1][:, s_], op=ALU.subtract)
+        def zsub2(i):
+            if i in Z_ON_G:
+                for t in range(4):
+                    s_ = slice(t * TOK, (t + 1) * TOK)
+                    nc.gpsimd.tensor_tensor(out=a[i, 0][:, s_], in0=a[i, 0][:, s_], in1=a[i, 1][:, s_], op=ALU.subtract)
+            else:
+                nc.vector.tensor_tensor(out=a[i, 0][:], in0=a[i, 0][:], in1=a[i, 1][:], op=ALU.subtract)
 
-        def widen_b(i, b):
-            if b == 0:
-                xw[i] = st.tile([P, SUB * D], BF16, name="xw", bufs=2)
-            nc.vector.tensor_tensor(out=xw[i][:, b * D : (b + 1) * D], in0=xby[i][:, b, :].bitcast(FP8), in1=scale[:], op=ALU.mult)
+        def widen2(i):
+            if i >= TILES:
+                return
+            xw[i] = st.tile([P, SUB * D], BF16, name="xw", bufs=2)
+            for h in range(2):
+                s_ = slice(h * 1024, (h + 1) * 1024)
+                nc.vector.tensor_tensor(
+                    out=xw[i][:, s_], in0=xby[i][:].rearrange("p b k -> p (b k)")[:, s_].bitcast(FP8), in1=scale[:], op=ALU.mult
+                )
 
-        def turn_b(i, b):
-            h = b // 2
-            if b % 2 == 0:
-                xps[i, h] = psum.tile([P, 2, 2, P], F32, name="xps", bufs=1)
-            words = xw[i][:, b * D : (b + 1) * D].bitcast(F32)
-            for u in range(2):
-                nc.tensor.transpose(xps[i, h][:, b % 2, u, :], words[:, u : D // 2 : 2], ident[:])
+        def turn2(i, h):
+            if i >= TILES:
+                return
+            xps[i, h] = psum.tile([P, 2, 2, P], F32, name="xps", bufs=XB)
+            for b in (0, 1):
+                c0 = (2 * h + b) * D
+                words = xw[i][:, c0 : c0 + D].bitcast(F32)
+                for u in range(2):
+                    nc.tensor.transpose(xps[i, h][:, b, u, :], words[:, u : D // 2 : 2], ident[:])
+
+        def empty2(i):
+            if i >= TILES:
+                return
+            empty_x(i, 0)
+            empty_x(i, 1)
 
         def flux_h(i, h):
             if h == 0:
@@ -289,59 +301,104 @@ def tile_learnedstencilwenostep_t_kernel(tc, x_bytes, x_scale, cs, ss, gamma, g,
             s_ = slice(h * 256, (h + 1) * 256)
             nc.vector.quantize_mx(out=pc[i][:, s_].bitcast(FP8X4), scales=psc[i][:, s_], in_=pg[i][:, h * 1024 : (h + 1) * 1024])
 
-        pq = []
-        tq = []
+        def vgain2(i, t):
+            if t == 0:
+                vv[i] = st.tile([P, 4 * TOK], F32, name="vv", bufs=2)
+            s_ = slice(t * TOK, (t + 1) * TOK)
+            e = VG[i] if not (VG[i] == 2 and t in VG3) else 0
+            if e == 0:
+                nc.vector.tensor_scalar(out=vv[i][:, s_], in0=qh[i][:, s_], scalar1=ghalf[:, t : t + 1], scalar2=gfull[:, t : t + 1], op0=ALU.mult, op1=ALU.add)
+            elif e == 1:
+                nc.scalar.activation(out=vv[i][:, s_], in_=qh[i][:, s_], func=ACT.Identity, scale=ghalf[:, t : t + 1], bias=gfull[:, t : t + 1])
+            else:
+                nc.gpsimd.tensor_scalar(out=vv[i][:, s_], in0=qh[i][:, s_], scalar1=ghalf[:, t : t + 1], scalar2=gfull[:, t : t + 1], op0=ALU.mult, op1=ALU.add)
 
-        def run_due(queue, now, all_=False):
-            rest = []
-            for due, fn, args in queue:
-                if due <= now or all_:
-                    fn(*args)
-                else:
-                    rest.append((due, fn, args))
-            queue[:] = rest
+        cnext = [0]
+        avail = [0]
 
-        def p_slot(p):
-            i, t = p // 4, p % 4
-            square(i, 0, t)
-            square(i, 1, t)
-            run_due(pq, p)
-            if i + XA < TILES:
-                widen_b(i + XA, t)
-                pq.append((p + 1, turn_b, (i + XA, t)))
-                if t == 1:
-                    pq.append((p + 2, empty_x, (i + XA, 0)))
-                if t == 3:
-                    pq.append((p + 2, empty_x, (i + XA, 1)))
-                    pq.append((p + 3, quant_x, (i + XA,)))
-            if t % 2 == 1:
-                h = t // 2
-                pq.append((p + 1, logh, (i, 0, h)))
-                pq.append((p + 1, logh, (i, 1, h)))
-                pq.append((p + ZL, zsubh, (i, h)))
-            if t == 3 and i + 4 < TILES:
-                load_x(i + 4)
+        def cands(n):
+            while cnext[0] < min(n, avail[0]):
+                cand(cnext[0] // 4, cnext[0] % 4)
+                cnext[0] += 1
 
-        def t_slot(q):
-            l, t = q // 4, q % 4
-            if q == 0:
-                cand(0, 0)
-            if q + 1 < navail:
-                cand((q + 1) // 4, (q + 1) % 4)
-            elif q + 1 < 4 * TILES:
-                tq.append((q + 1, cand, ((q + 1) // 4, (q + 1) % 4)))
-            blend_m(l, t)
-            run_due(tq, q)
-            blend_q(l, t)
-            tq.append((q + 1, vgain, (l, t)))
-            if t == 3:
-                f = q + (FL if l in V_ON_S else 1)
-                tq.append((f, flux_h, (l, 0)))
-                tq.append((f + 1, flux_h, (l, 1)))
-                tq.append((f + 1, quant_ph, (l, 0)))
-                tq.append((f + 2, quant_ph, (l, 1)))
-                for b in range(SUB):
-                    tq.append((f + 2 + b, div, (l, b)))
+        state = {"ln": None, "o": None, "n": 1, "l": -1}
+        wq = []
+
+        def weights_work(n):
+            for _ in range(n):
+                if wq:
+                    fn, ar, kw = wq.pop(0)
+                    fn(*ar, **kw)
+
+        def step(i, l, sig=(), wn=0):
+            j = state["ln"]
+            lo = state["o"]
+            n = state["n"] if i is not None else TILES
+            nl = l + 1 if l is not None else (state["l"] + 1)
+            if j is not None:
+                logk(j, 0)
+                logk(j, 1)
+            for x in sig:
+                if x != j:
+                    sigmoid(x)
+            if l is not None:
+                cands(4 * l + 2)
+                blend_m(l, 0)
+                blend_m(l, 1)
+                turn2(n, 0)
+                blend_q(l, 0)
+                vgain2(l, 0)
+                cands(4 * l + 3)
+                blend_m(l, 2)
+                blend_q(l, 1)
+                vgain2(l, 1)
+                cands(4 * l + 4)
+                empty_x(n, 0) if n < TILES else None
+                blend_m(l, 3)
+                turn2(n, 1)
+                blend_q(l, 2)
+                vgain2(l, 2)
+                blend_q(l, 3)
+                vgain2(l, 3)
+                empty_x(n, 1) if n < TILES else None
+            if j is not None and ZPOS == 0:
+                zsub2(j)
+            if j in sig:
+                sigmoid(j)
+            avail[0] += 4 * len(sig)
+            if i is None:
+                cands(4 * nl + 2)
+            for t in range(4):
+                if i is not None:
+                    square(i, 0, t)
+                    square(i, 1, t)
+                if l is None and t in (1, 3) and n < TILES:
+                    turn2(n, t // 2)
+                    empty_x(n, t // 2)
+                if i is not None and t == 2:
+                    cands(4 * nl + 2)
+                if lo is not None:
+                    div(lo, t)
+            if i is not None and n < TILES:
+                quant_x(n)
+                if i + 4 < TILES:
+                    load_x(i + 4)
+            if l is not None:
+                flux_h(l, 0)
+            if j is not None and ZPOS == 1:
+                zsub2(j)
+            weights_work(wn)
+            if l is not None:
+                flux_h(l, 1)
+                quant_ph(l, 0)
+                quant_ph(l, 1)
+            if i is not None:
+                widen2(n + 1)
+                state["n"] = n + 1
+            if l is not None:
+                state["l"] = l
+            state["ln"] = i
+            state["o"] = l
 
         def wprep(name, raw, eng, **kw):
             w_group(name, wraw[raw], eng, **kw)
@@ -349,65 +406,36 @@ def tile_learnedstencilwenostep_t_kernel(tc, x_bytes, x_scale, cs, ss, gamma, g,
         dummy = keep.tile([P, 1], F32, name="dummy")
         nc.scalar.activation(out=dummy[:], in_=half[:], func=ACT.Ln)
         wprep("s1", "s1", "s")
+        xw[0] = st.tile([P, SUB * D], BF16, name="xw", bufs=2)
         for b in range(SUB):
-            widen_b(0, b)
-            turn_b(0, b)
+            nc.vector.tensor_tensor(out=xw[0][:, b * D : (b + 1) * D], in0=xby[0][:, b, :].bitcast(FP8), in1=scale[:, :D], op=ALU.mult)
             if b == 1:
-                wprep("s0", "s0", "v")
-        empty_x(0, 0)
-        w_quant("s0")
-        empty_x(0, 1)
-        quant_x(0)
+                turn2(0, 0)
+        turn2(0, 1)
+        wprep("s0", "s0", "v")
+        empty2(0)
         w_quant("s1")
+        w_quant("s0")
+        quant_x(0)
+        nc.vector.tensor_copy(out=scale[:, D:], in_=scale[:, :D])
         constants_s()
         constants_v()
+        widen2(1)
         load_w("c0", cs[0], nc.sync)
         load_x(2)
         load_w("dv", dv, nc.sync)
         load_x(3)
-        for x in range(1, XA):
-            for b in range(SUB):
-                widen_b(x, b)
-                turn_b(x, b)
-                if b == 2:
-                    empty_x(x, 0)
-            empty_x(x, 1)
-            quant_x(x)
-        WORK = {
-            2: [(wprep, ("c1", "c1", "v"), {}), ],
-            4: [(w_quant, ("c1",), {})],
-            5: [(wprep, ("c0", "c0", "v"), {})],
-            7: [(w_quant, ("c0",), {})],
-            8: [(wprep, ("n0", "c0", "v"), {"sign": -1.0})],
-            10: [(w_quant, ("n0",), {})],
-            11: [(wprep, ("dv", "dv", "v"), {"permute": False})],
-            13: [(w_quant, ("dv",), {})],
-        }
-        q = 0
-        navail = 0
-        p = 0
-        for gi, n in enumerate(GSIZE):
-            for s in range(4 * n):
-                p_slot(p)
-                for fn, ar, kw in WORK.get(p, []):
-                    fn(*ar, **kw)
-                p += 1
-                if gi > 0:
-                    target = QS[gi] + (s + 1) * QN[gi] // (4 * n)
-                    while q < min(target, 4 * (p // 4 - 0) ) and q < navail:
-                        t_slot(q)
-                        q += 1
-            run_due(pq, 0, True)
-            first = p // 4 - n
-            for i in range(first, first + n):
-                sigmoid(i)
-            navail = 4 * (first + n)
-            if gi + 1 < len(GSIZE):
-                while q < QS[gi + 1]:
-                    t_slot(q)
-                    q += 1
-        while q < 4 * TILES:
-            t_slot(q)
-            q += 1
-        for s in range(12):
-            run_due(tq, q + s)
+        wq += [
+            (wprep, ("c1", "c1", WE[0]), {}),
+            (w_quant, ("c1",), {}),
+            (wprep, ("c0", "c0", WE[1]), {}),
+            (w_quant, ("c0",), {}),
+            (wprep, ("n0", "c0", WE[2]), {"sign": -1.0}),
+            (w_quant, ("n0",), {}),
+            (wprep, ("dv", "dv", WE[3]), {"permute": False}),
+            (w_quant, ("dv",), {}),
+        ]
+        for what in PROGRAM:
+            step(*what)
+        for b in range(SUB):
+            div(state["o"], b)

@@ -20,16 +20,50 @@ FP8X4 = mybir.dt.float8_e4m3fn_x4
 ALU = mybir.AluOpType
 ACT = mybir.ActivationFunctionType
 
-E_ON_V = range(1, 8)
-PROGRAM = ((0,None,(),2),(1,None,(),2),(2,None,(),2),(None,None,(0,1,2),2),(3,0),(4,1),(5,None),(None,2,(3,4,5)),(6,3),(7,4),(None,5,(6,7)),(None,6),(None,7))
-VG = (2,2,2,2,2,2,2,2)
-VG3 = ()
-ZPOS = 0
-Z_ON_G = ()
-WE = 'vvnv'
-WN = 2
-XB = 1
-O_ON_V = ()
+STEPS = ((0, None, (), 3), (1, None, (), 3), (None, None, (0, 1), 8), (2, 0, (), 0), (3, None, (), 0), (4, 1, (), 0), (None, None, (2, 3, 4), 0), (5, 2, (), 0), (6, 3, (), 0), (None, 4, (5, 6), 0), (7, 5, (), 0), (None, 6, (7,), 0), (None, 7, (), 0))
+SPS = 3
+DPS = 2
+QPS = 2
+XPS = 1
+RUN = 2
+VG = (2, 2, 2, 2, 2, 2, 2, 2)
+EXS = (0,)
+ZL = 0
+WORDER = 0
+LATX = 0.07
+LATP = 0.17
+OV = ()
+
+
+def issue(streams, clock):
+    done = {}
+    table = [None]
+    heads = [0] * len(streams)
+    left = sum(len(s) for s in streams)
+    while left:
+        best = None
+        for n, s in enumerate(streams):
+            if heads[n] == len(s):
+                continue
+            engine, cost, needs, gives, fn = s[heads[n]]
+            t = clock.get(engine, 0.0)
+            ok = True
+            for x in needs:
+                if x not in done:
+                    ok = False
+                    break
+                e, d = done[x]
+                t = max(t, d + (0.18 if e == engine and e == "v" else 0.0 if e == engine else LATP if e == "t" else LATX))
+            if ok and (best is None or t < best[0]):
+                best = (t, n)
+        t, n = best
+        engine, cost, needs, gives, fn = streams[n][heads[n]]
+        fn()
+        heads[n] += 1
+        left -= 1
+        clock[engine] = t + cost
+        if gives is not None:
+            done[gives] = (engine, t + cost)
 
 
 def tile_learnedstencilwenostep_t_kernel(tc, x_bytes, x_scale, cs, ss, gamma, g, dv, out):
@@ -39,121 +73,130 @@ def tile_learnedstencilwenostep_t_kernel(tc, x_bytes, x_scale, cs, ss, gamma, g,
         wst = ctx.enter_context(tc.tile_pool(name="wst", bufs=2))
         st = ctx.enter_context(tc.tile_pool(name="st", bufs=2))
         psum = ctx.enter_context(tc.psum_pool(name="psum", bufs=1))
-        ctx.enter_context(tc.manual_schedule(engines={mybir.EngineType.Activation}))
+        ctx.enter_context(tc.manual_schedule())
+
+        loads, vec, act, gps, sfeed, vfeed = [], [], [], [], [], []
 
         scale = keep.tile([P, 2 * D], F32, name="scale")
-        xby = {}
-
-        def load_x(i):
-            t = st.tile([P, SUB, D], U8, name="xby", bufs=4)
-            rows = x_bytes[i * TOK : (i + 1) * TOK, :]
-            nc.sync.dma_start(out=t[:], in_=rows.rearrange("(p b) k -> p b k", b=SUB))
-            xby[i] = t
-
-        wraw = {}
-
-        def load_w(name, src, eng):
-            t = wst.tile([P, 4, 512], BF16, name="wraw", bufs=3)
-            eng.dma_start(out=t[:], in_=src.rearrange("(p j) c -> p j c", j=4))
-            wraw[name] = t
-
         gam = keep.tile([P, 2, 4], BF16, name="gam")
         gcol = keep.tile([P, 4], BF16, name="gcol")
-        load_x(0)
-        nc.scalar.dma_start(out=scale[:, :D], in_=x_scale.rearrange("o k -> (o k)").partition_broadcast(P))
-        load_w("s1", ss[1], nc.sync)
-        load_w("s0", ss[0], nc.sync)
-        nc.scalar.dma_start(out=gam[:], in_=gamma.rearrange("k (p t) -> p k t", t=4))
-        nc.scalar.dma_start(out=gcol[:], in_=g.rearrange("(p t) -> p t", t=4))
-        load_x(1)
-        load_w("c1", cs[1], nc.sync)
-
         ident = keep.tile([P, P], F32, name="ident")
-        make_identity(nc, ident[:])
         half = keep.tile([P, 1], F32, name="half")
-        nc.vector.memset(half[:], 0.5)
-
+        dummy = keep.tile([P, 1], F32, name="dummy")
         lgam = keep.tile([P, 2, 4], F32, name="lgam")
         lrho = keep.tile([P, 4], F32, name="lrho")
         gfull = keep.tile([P, 4], F32, name="gfull")
         ghalf = keep.tile([P, 4], F32, name="ghalf")
+        make_identity(nc, ident[:])
+        nc.vector.memset(half[:], 0.5)
+        nc.scalar.activation(out=dummy[:], in_=half[:], func=ACT.Ln)
+        codes, scales, wraw, wgrp = {}, {}, {}, {}
+        for w in ("s0", "s1", "c1", "c0", "n0", "dv"):
+            codes[w] = keep.tile([P, 512], U32, name="codes_" + w, align_bytes=64)
+            scales[w] = keep.tile([P, 512], U8, name="scales_" + w, align_bytes=64)
+        xby, xw, xps, xg, xc, xs = {}, {}, {}, {}, {}, {}
+        a, qh, vv, dps, qps, sps = {}, {}, {}, {}, {}, {}
+        pg, pc, psc, osb = {}, {}, {}, {}
 
-        def constants_s():
-            nc.scalar.activation(out=lgam[:], in_=gam[:], func=ACT.Ln)
+        def load_x(i):
+            def f():
+                xby[i] = st.tile([P, SUB, D], U8, name="xby", bufs=4)
+                rows = x_bytes[i * TOK : (i + 1) * TOK, :]
+                nc.sync.dma_start(out=xby[i][:], in_=rows.rearrange("(p b) k -> p b k", b=SUB))
 
-        def constants_v():
-            nc.vector.tensor_tensor(out=lrho[:], in0=lgam[:, 1, :], in1=lgam[:, 0, :], op=ALU.subtract)
-            nc.vector.tensor_copy(out=gfull[:], in_=gcol[:])
-            nc.vector.tensor_scalar(out=ghalf[:], in0=gcol[:], scalar1=0.5, scalar2=None, op0=ALU.mult)
+            loads.append(("dma", 0.5, [("xw", i - 4, 1)] if i >= 4 else [], ("xby", i), f))
 
-        wgrp = {}
-        codes = {}
-        scales = {}
+        def load_w(w, src):
+            def f():
+                wraw[w] = wst.tile([P, 4, 512], BF16, name="wraw", bufs=3)
+                nc.sync.dma_start(out=wraw[w][:], in_=src.rearrange("(p j) c -> p j c", j=4))
 
-        def w_group(name, raw, eng, sign=1.0, permute=True):
-            grp = wst.tile([P, 2048], BF16, name="wgrp", bufs=3, align_bytes=64)
-            if permute:
-                o = grp[:].rearrange("p (t m j) -> p t m j", t=4, j=4)
-                i = raw[:].rearrange("p j (m t) -> p t m j", t=4)
-            else:
-                o = grp[:].rearrange("p (c j) -> p c j", j=4)
-                i = raw[:].rearrange("p j c -> p c j")
-            if eng == "v":
-                if sign == 1.0:
+            k = len(wq)
+            loads.append(("dma", 1.0, [("wg", wq[k - 3])] if k >= 3 else [], ("wraw", w), f))
+            wq.append(w)
+
+        wq = []
+
+        def load_scale():
+            nc.scalar.dma_start(out=scale[:, :D], in_=x_scale.rearrange("o k -> (o k)").partition_broadcast(P))
+            nc.scalar.dma_start(out=gam[:], in_=gamma.rearrange("k (p t) -> p k t", t=4))
+            nc.scalar.dma_start(out=gcol[:], in_=g.rearrange("(p t) -> p t", t=4))
+
+        def weight(w, engine):
+            def group():
+                wgrp[w] = wst.tile([P, 2048], BF16, name="wgrp", bufs=3, align_bytes=64)
+                if w == "n0":
+                    nc.vector.tensor_scalar(out=wgrp[w][:], in0=wgrp["c0"][:], scalar1=-1.0, scalar2=None, op0=ALU.mult)
+                    return
+                if w == "dv":
+                    o = wgrp[w][:].rearrange("p (c j) -> p c j", j=4)
+                    i = wraw[w][:].rearrange("p j c -> p c j")
+                else:
+                    o = wgrp[w][:].rearrange("p (t m j) -> p t m j", t=4, j=4)
+                    i = wraw[w][:].rearrange("p j (m t) -> p t m j", t=4)
+                if engine == "v":
                     nc.vector.tensor_copy(out=o, in_=i)
                 else:
-                    nc.vector.tensor_scalar(out=o, in0=i, scalar1=sign, scalar2=None, op0=ALU.mult)
-            elif eng == "n":
-                nc.vector.tensor_scalar(out=grp[:], in0=wgrp["c0"][:], scalar1=-1.0, scalar2=None, op0=ALU.mult)
-            elif eng == "g":
-                nc.gpsimd.tensor_scalar(out=o, in0=i, scalar1=sign, scalar2=0.0, op0=ALU.mult, op1=ALU.add)
-            elif eng == "s":
-                if sign == 1.0:
                     nc.scalar.copy(out=o, in_=i)
-                else:
-                    nc.scalar.activation(out=o, in_=i, func=ACT.Copy, scale=sign)
-            wgrp[name] = grp
 
-        def w_quant(name):
-            codes[name] = keep.tile([P, 512], U32, name="codes_" + name, align_bytes=64)
-            scales[name] = keep.tile([P, 512], U8, name="scales_" + name, align_bytes=64)
-            nc.vector.quantize_mx(out=codes[name][:].bitcast(FP8X4), scales=scales[name][:], in_=wgrp[name][:])
+            cost = 0.46 if w == "n0" else 1.07 if engine == "v" else 2.0
+            need = ("wg", "c0") if w == "n0" else ("wraw", w)
+            (vec if engine == "v" else act).append((engine, cost, [need], ("wg", w), group))
 
-        xw = {}
-        xps = {}
-        xg = {}
-        xc = {}
-        xs = {}
+        def weight_quant(w):
+            def f():
+                nc.vector.quantize_mx(out=codes[w][:].bitcast(FP8X4), scales=scales[w][:], in_=wgrp[w][:])
 
-        def widen(i):
-            t = st.tile([P, SUB * D], BF16, name="xw", bufs=2)
-            for b in range(SUB):
-                nc.vector.tensor_tensor(out=t[:, b * D : (b + 1) * D], in0=xby[i][:, b, :].bitcast(FP8), in1=scale[:], op=ALU.mult)
-            xw[i] = t
+            vec.append(("v", 0.48, [("wg", w)], ("w", w), f))
+
+        def widen(i, h, wide):
+            def f():
+                if h == 0:
+                    xw[i] = st.tile([P, SUB * D], BF16, name="xw", bufs=2)
+                src = xby[i][:].rearrange("p b k -> p (b k)")
+                n = 2 * D if wide else D
+                for c in range(h * 2 * D, (h + 1) * 2 * D, n):
+                    nc.vector.tensor_tensor(
+                        out=xw[i][:, c : c + n], in0=src[:, c : c + n].bitcast(FP8), in1=scale[:, :n], op=ALU.mult
+                    )
+
+            needs = [("xby", i)] + ([("turn", i - 2, 1)] if i >= 2 else []) + ([("scale2",)] if wide else [("scale",)])
+            vec.append(("v", 0.88 if wide else 0.91, needs, ("xw", i, h), f))
 
         def turn(i, h):
-            ps = psum.tile([P, 2, 2, P], F32, name="xps", bufs=1)
-            for b in range(2):
-                c0 = (2 * h + b) * D
-                words = xw[i][:, c0 : c0 + D].bitcast(F32)
-                for u in range(2):
-                    nc.tensor.transpose(ps[:, b, u, :], words[:, u : D // 2 : 2], ident[:])
-            xps[i, h] = ps
+            def f():
+                xps[i, h] = psum.tile([P, 2, 2, P], F32, name="xps", bufs=XPS)
+                for b in (0, 1):
+                    c0 = (2 * h + b) * D
+                    words = xw[i][:, c0 : c0 + D].bitcast(F32)
+                    for u in range(2):
+                        nc.tensor.transpose(xps[i, h][:, b, u, :], words[:, u : D // 2 : 2], ident[:])
 
-        def empty_x(i, h):
-            if h == 0:
-                xg[i] = st.tile([P, TOK * 4], BF16, name="xg", bufs=2, align_bytes=64)
-            o = xg[i][:, h * 1024 : (h + 1) * 1024].bitcast(F32).rearrange("p (b n u) -> p b n u", b=2, u=2)
-            src = xps[i, h][:].rearrange("p b u n -> p b n u")
-            if i in E_ON_V:
-                nc.vector.tensor_copy(out=o, in_=src)
-            else:
-                nc.scalar.copy(out=o, in_=src)
+            k = 2 * i + h - XPS
+            vfeed.append(("t", 0.45, [("xw", i, h)] + ([("xg", k // 2, k % 2)] if k >= 0 else []), ("turn", i, h), f))
+
+        def empty(i, h):
+            def f():
+                if h == 0:
+                    xg[i] = st.tile([P, TOK * 4], BF16, name="xg", bufs=2, align_bytes=64)
+                o = xg[i][:, h * 1024 : (h + 1) * 1024].bitcast(F32).rearrange("p (b n u) -> p b n u", b=2, u=2)
+                src = xps[i, h][:].rearrange("p b u n -> p b n u")
+                if i in EXS:
+                    nc.scalar.copy(out=o, in_=src)
+                else:
+                    nc.vector.tensor_copy(out=o, in_=src)
+
+            turn(i, h)
+            e = "s" if i in EXS else "v"
+            (act if i in EXS else vec).append((e, 0.455, [("turn", i, h)] + ([("xq", i - 2)] if i >= 2 else []), ("xg", i, h), f))
 
         def quant_x(i):
-            xc[i] = st.tile([P, TOK], U32, name="xc", bufs=TILES, align_bytes=64)
-            xs[i] = st.tile([P, TOK], U8, name="xs", bufs=TILES, align_bytes=64)
-            nc.vector.quantize_mx(out=xc[i][:].bitcast(FP8X4), scales=xs[i][:], in_=xg[i][:])
+            def f():
+                xc[i] = keep.tile([P, TOK], U32, name="xc%d" % i, align_bytes=64)
+                xs[i] = keep.tile([P, TOK], U8, name="xs%d" % i, align_bytes=64)
+                nc.vector.quantize_mx(out=xc[i][:].bitcast(FP8X4), scales=xs[i][:], in_=xg[i][:])
+
+            vec.append(("v", 0.48, [("xg", i, 0), ("xg", i, 1)], ("xq", i), f))
 
         def mm(ps, w, t, i, start, stop):
             nc.tensor.matmul_mx(
@@ -166,276 +209,281 @@ def tile_learnedstencilwenostep_t_kernel(tc, x_bytes, x_scale, cs, ss, gamma, g,
                 stop=stop,
             )
 
-        a = {}
+        ring = []
+
+        def ring_needs():
+            n = len(ring)
+            ring.append(n)
+            return n, ([("sfree", n - SPS)] if n >= SPS else [])
+
+        arel = {}
 
         def square(i, k, t):
-            if t == 0:
-                a[i, k] = st.tile([P, 4 * TOK], F32, name="a%d" % k, bufs=7 if k == 0 else 2)
-            ps = psum.tile([P, TOK], F32, name="sps", tag="sps", bufs=3)
-            mm(ps, "s%d" % k, t, i, True, True)
-            nc.scalar.activation(out=a[i, k][:, t * TOK : (t + 1) * TOK], in_=ps[:], func=ACT.Square)
+            n, needs = ring_needs()
+
+            def f():
+                sps[n] = psum.tile([P, TOK], F32, name="sps", bufs=SPS)
+                mm(sps[n], "s%d" % k, t, i, True, True)
+
+            def h():
+                if t == 0:
+                    a[i, k] = st.tile([P, 4 * TOK], F32, name="a%d" % k, bufs=7 if k == 0 else 2)
+                nc.scalar.activation(out=a[i, k][:, t * TOK : (t + 1) * TOK], in_=sps[n][:], func=ACT.Square)
+
+            sfeed.append(("t", 0.225, needs + [("xq", i), ("w", "s%d" % k)], ("smm", n), f))
+            more = []
+            if t == 0 and k == 1 and i >= 2:
+                more = [("z", i - 2)]
+            if t == 0 and k == 0 and i >= 7:
+                more = [("m", i - 7, 3)]
+            act.append(("s", 0.447, [("smm", n)] + more, ("sfree", n), h))
+
+        mode = [None]
+
+        def table(m):
+            c = 0.0 if mode[0] == m else 1.3
+            mode[0] = m
+            return c
 
         def log(i, k):
-            nc.scalar.activation(out=a[i, k][:], in_=a[i, k][:], func=ACT.Ln, bias=half[:, 0:1])
+            def f():
+                z = a[i, k][:]
+                nc.scalar.activation(out=z, in_=z, func=ACT.Ln, bias=half[:, 0:1])
 
-        def zsub(i):
-            nc.vector.tensor_tensor(out=a[i, 0][:], in0=a[i, 0][:], in1=a[i, 1][:], op=ALU.subtract)
+            act.append(("s", 1.73 + table("ln"), [], ("ln", i, k), f))
+
+        def difference(i):
+            def f():
+                nc.vector.tensor_tensor(out=a[i, 0][:], in0=a[i, 0][:], in1=a[i, 1][:], op=ALU.subtract)
+
+            vec.append(("v", 1.73, [("ln", i, 1)], ("z", i), f))
 
         def sigmoid(i):
             for t in range(4):
-                z = a[i, 0][:, t * TOK : (t + 1) * TOK]
-                nc.scalar.activation(out=z, in_=z, func=ACT.Sigmoid, bias=lrho[:, t : t + 1], scale=2.0)
 
-        qh = {}
-        dps = {}
-        qps = {}
-        vv = {}
-        pg = {}
-        pc = {}
-        psc = {}
+                def f(t=t):
+                    z = a[i, 0][:, t * TOK : (t + 1) * TOK]
+                    nc.scalar.activation(out=z, in_=z, func=ACT.Sigmoid, bias=lrho[:, t : t + 1], scale=2.0)
+
+                act.append(("s", 0.447 + table("sig"), [("z", i), ("lrho",)], ("sig", i, t), f))
 
         def cand(i, t):
-            dps[i, t] = psum.tile([P, TOK], F32, name="dps", bufs=2)
-            mm(dps[i, t], "c1", t, i, True, False)
-            mm(dps[i, t], "n0", t, i, False, True)
-            qps[i, t] = psum.tile([P, TOK], F32, name="qps", bufs=2)
-            mm(qps[i, t], "c0", t, i, True, True)
+            n = 4 * i + t
+
+            def fd():
+                dps[n] = psum.tile([P, TOK], F32, name="dps", bufs=DPS)
+                mm(dps[n], "c1", t, i, True, False)
+                mm(dps[n], "n0", t, i, False, True)
+
+            def fq():
+                qps[n] = psum.tile([P, TOK], F32, name="qps", bufs=QPS)
+                mm(qps[n], "c0", t, i, True, True)
+
+            kd, kq = n - DPS, n - QPS
+            vfeed.append(("t", 0.45, [("w", "n0"), ("w", "c1"), ("xq", i)] + ([("m", kd // 4, kd % 4)] if kd >= 0 else []), ("d", i, t), fd))
+            vfeed.append(("t", 0.225, [("w", "c0"), ("xq", i)] + ([("q", kq // 4, kq % 4)] if kq >= 0 else []), ("qp", i, t), fq))
 
         def blend_m(i, t):
-            if t == 0:
-                qh[i] = st.tile([P, 4 * TOK], F32, name="qh", bufs=2)
-            s_ = slice(t * TOK, (t + 1) * TOK)
-            nc.vector.tensor_tensor(out=qh[i][:, s_], in0=a[i, 0][:, s_], in1=dps[i, t][:], op=ALU.mult)
+            def f():
+                if t == 0:
+                    qh[i] = st.tile([P, 4 * TOK], F32, name="qh", bufs=2)
+                s_ = slice(t * TOK, (t + 1) * TOK)
+                nc.vector.tensor_tensor(out=qh[i][:, s_], in0=a[i, 0][:, s_], in1=dps[4 * i + t][:], op=ALU.mult)
+
+            cand(i, t)
+            vec.append(("v", 0.455, [("d", i, t), ("sig", i, t)], ("m", i, t), f))
 
         def blend_q(i, t):
-            s_ = slice(t * TOK, (t + 1) * TOK)
-            nc.vector.tensor_tensor(out=qh[i][:, s_], in0=qh[i][:, s_], in1=qps[i, t][:], op=ALU.add)
+            def f():
+                s_ = slice(t * TOK, (t + 1) * TOK)
+                nc.vector.tensor_tensor(out=qh[i][:, s_], in0=qh[i][:, s_], in1=qps[4 * i + t][:], op=ALU.add)
 
-        def flux(i):
-            pg[i] = st.tile([P, TOK * 4], BF16, name="pg", bufs=2, align_bytes=64)
-            o = pg[i][:].rearrange("p (c i t) -> p c t i", i=2, t=4)
-            q_ = qh[i][:].rearrange("p (t c i) -> p c t i", t=4, i=2)
-            v_ = vv[i][:].rearrange("p (t c i) -> p c t i", t=4, i=2)
-            nc.vector.tensor_tensor(out=o, in0=q_, in1=v_, op=ALU.mult)
+            def v():
+                if t == 0:
+                    vv[i] = st.tile([P, 4 * TOK], F32, name="vv", bufs=2)
+                s_ = slice(t * TOK, (t + 1) * TOK)
+                e = VG[i]
+                if e == 1:
+                    nc.scalar.activation(out=vv[i][:, s_], in_=qh[i][:, s_], func=ACT.Identity, scale=ghalf[:, t : t + 1], bias=gfull[:, t : t + 1])
+                else:
+                    eng = nc.gpsimd if e == 2 else nc.vector
+                    eng.tensor_scalar(
+                        out=vv[i][:, s_], in0=qh[i][:, s_], scalar1=ghalf[:, t : t + 1], scalar2=gfull[:, t : t + 1], op0=ALU.mult, op1=ALU.add
+                    )
 
-        def quant_p(i):
-            pc[i] = st.tile([P, TOK], U32, name="pc", bufs=2, align_bytes=64)
-            psc[i] = st.tile([P, TOK], U8, name="psc", bufs=2, align_bytes=64)
-            nc.vector.quantize_mx(out=pc[i][:].bitcast(FP8X4), scales=psc[i][:], in_=pg[i][:])
+            vec.append(("v", 0.455, [("qp", i, t), ("m", i, t)], ("q", i, t), f))
+            e = "vsg"[VG[i]]
+            late = (e, {"v": 0.24, "s": 0.447, "g": 0.55}[e], [("q", i, t), ("gain",)] + ([("pg", i - 2, 1)] if i >= 2 else []), ("v", i, t), v)
+            if e == "v":
+                return late
+            (gps if e == "g" else act).append(late)
+            return None
 
-        osb = {}
+        def flux(i, h):
+            def f():
+                if h == 0:
+                    pg[i] = st.tile([P, TOK * 4], BF16, name="pg", bufs=2, align_bytes=64)
+                o = pg[i][:, h * 1024 : (h + 1) * 1024].rearrange("p (c i t) -> p c t i", i=RUN, t=4)
+                q_ = qh[i][:].rearrange("p (t h c i) -> p h c t i", t=4, i=RUN, h=2)[:, h]
+                v_ = vv[i][:].rearrange("p (t h c i) -> p h c t i", t=4, i=RUN, h=2)[:, h]
+                nc.vector.tensor_tensor(out=o, in0=q_, in1=v_, op=ALU.mult)
 
-        def div(i, b):
-            if b == 0:
-                osb[i] = st.tile([P, SUB, D], F32, name="osb", bufs=2)
-            ps = psum.tile([P, D], F32, name="ops", tag="sps", bufs=3)
-            nc.tensor.matmul_mx(
-                out=ps[:],
-                lhsT=pc[i][:, b * P : (b + 1) * P].bitcast(FP8X4),
-                lhsT_scale=psc[i][:, b * P : (b + 1) * P],
-                rhs=codes["dv"][:].bitcast(FP8X4),
-                rhs_scale=scales["dv"][:],
-                start=True,
-                stop=True,
-            )
-            if (i, b) in O_ON_V:
-                nc.vector.tensor_copy(out=osb[i][:, b, :], in_=ps[:])
-            else:
-                nc.scalar.copy(out=osb[i][:, b, :], in_=ps[:])
-            rows = out[i * TOK : (i + 1) * TOK, :].rearrange("(p b) d -> p b d", b=SUB)
-            if i == TILES - 1:
-                nc.sync.dma_start(out=rows[:, b, :], in_=osb[i][:, b, :])
-            elif b == SUB - 1:
-                nc.sync.dma_start(out=rows, in_=osb[i][:])
+            vec.append(("v", 0.88, [("v", i, t) for t in range(4)], ("pg", i, h), f))
 
-        def logk(i, k):
-            z = a[i, k][:]
-            nc.scalar.activation(out=z, in_=z, func=ACT.Ln, bias=half[:, 0:1])
-
-        def zsub2(i):
-            if i in Z_ON_G:
-                for t in range(4):
-                    s_ = slice(t * TOK, (t + 1) * TOK)
-                    nc.gpsimd.tensor_tensor(out=a[i, 0][:, s_], in0=a[i, 0][:, s_], in1=a[i, 1][:, s_], op=ALU.subtract)
-            else:
-                nc.vector.tensor_tensor(out=a[i, 0][:], in0=a[i, 0][:], in1=a[i, 1][:], op=ALU.subtract)
-
-        def widen2(i):
-            if i >= TILES:
-                return
-            xw[i] = st.tile([P, SUB * D], BF16, name="xw", bufs=2)
-            for h in range(2):
-                s_ = slice(h * 1024, (h + 1) * 1024)
-                nc.vector.tensor_tensor(
-                    out=xw[i][:, s_], in0=xby[i][:].rearrange("p b k -> p (b k)")[:, s_].bitcast(FP8), in1=scale[:], op=ALU.mult
+        def quant_p(i, h):
+            def f():
+                if h == 0:
+                    pc[i] = st.tile([P, TOK], U32, name="pc", bufs=2, align_bytes=64)
+                    psc[i] = st.tile([P, TOK], U8, name="psc", bufs=2, align_bytes=64)
+                s_ = slice(h * 256, (h + 1) * 256)
+                nc.vector.quantize_mx(
+                    out=pc[i][:, s_].bitcast(FP8X4), scales=psc[i][:, s_], in_=pg[i][:, h * 1024 : (h + 1) * 1024]
                 )
 
-        def turn2(i, h):
-            if i >= TILES:
-                return
-            xps[i, h] = psum.tile([P, 2, 2, P], F32, name="xps", bufs=XB)
-            for b in (0, 1):
-                c0 = (2 * h + b) * D
-                words = xw[i][:, c0 : c0 + D].bitcast(F32)
-                for u in range(2):
-                    nc.tensor.transpose(xps[i, h][:, b, u, :], words[:, u : D // 2 : 2], ident[:])
+            vec.append(("v", 0.26, [("pg", i, h)] + ([("dmm", i - 2, 3)] if i >= 2 else []), ("pq", i, h), f))
 
-        def empty2(i):
-            if i >= TILES:
-                return
-            empty_x(i, 0)
-            empty_x(i, 1)
+        def div(i, b):
+            n, needs = ring_needs()
 
-        def flux_h(i, h):
-            if h == 0:
-                pg[i] = st.tile([P, TOK * 4], BF16, name="pg", bufs=2, align_bytes=64)
-            o = pg[i][:, h * 1024 : (h + 1) * 1024].rearrange("p (c i t) -> p c t i", i=2, t=4)
-            q_ = qh[i][:].rearrange("p (t h c i) -> p h c t i", t=4, i=2, h=2)[:, h]
-            v_ = vv[i][:].rearrange("p (t h c i) -> p h c t i", t=4, i=2, h=2)[:, h]
-            nc.vector.tensor_tensor(out=o, in0=q_, in1=v_, op=ALU.mult)
+            def f():
+                sps[n] = psum.tile([P, D], F32, name="sps", bufs=SPS)
+                nc.tensor.matmul_mx(
+                    out=sps[n][:],
+                    lhsT=pc[i][:, b * P : (b + 1) * P].bitcast(FP8X4),
+                    lhsT_scale=psc[i][:, b * P : (b + 1) * P],
+                    rhs=codes["dv"][:].bitcast(FP8X4),
+                    rhs_scale=scales["dv"][:],
+                    start=True,
+                    stop=True,
+                )
 
-        def quant_ph(i, h):
-            if h == 0:
-                pc[i] = st.tile([P, TOK], U32, name="pc", bufs=2, align_bytes=64)
-                psc[i] = st.tile([P, TOK], U8, name="psc", bufs=2, align_bytes=64)
-            s_ = slice(h * 256, (h + 1) * 256)
-            nc.vector.quantize_mx(out=pc[i][:, s_].bitcast(FP8X4), scales=psc[i][:, s_], in_=pg[i][:, h * 1024 : (h + 1) * 1024])
+            def h():
+                if b == 0:
+                    osb[i] = st.tile([P, SUB, D], F32, name="osb", bufs=2)
+                nc.scalar.copy(out=osb[i][:, b, :], in_=sps[n][:])
 
-        def vgain2(i, t):
-            if t == 0:
-                vv[i] = st.tile([P, 4 * TOK], F32, name="vv", bufs=2)
-            s_ = slice(t * TOK, (t + 1) * TOK)
-            e = VG[i] if not (VG[i] == 2 and t in VG3) else 0
-            if e == 0:
-                nc.vector.tensor_scalar(out=vv[i][:, s_], in0=qh[i][:, s_], scalar1=ghalf[:, t : t + 1], scalar2=gfull[:, t : t + 1], op0=ALU.mult, op1=ALU.add)
-            elif e == 1:
-                nc.scalar.activation(out=vv[i][:, s_], in_=qh[i][:, s_], func=ACT.Identity, scale=ghalf[:, t : t + 1], bias=gfull[:, t : t + 1])
-            else:
-                nc.gpsimd.tensor_scalar(out=vv[i][:, s_], in0=qh[i][:, s_], scalar1=ghalf[:, t : t + 1], scalar2=gfull[:, t : t + 1], op0=ALU.mult, op1=ALU.add)
+            rows = out[i * TOK : (i + 1) * TOK, :].rearrange("(p b) d -> p b d", b=SUB)
 
-        cnext = [0]
-        avail = [0]
+            def s():
+                if i == TILES - 1:
+                    nc.sync.dma_start(out=rows[:, b, :], in_=osb[i][:, b, :])
+                else:
+                    nc.sync.dma_start(out=rows, in_=osb[i][:])
 
-        def cands(n):
-            while cnext[0] < min(n, avail[0]):
-                cand(cnext[0] // 4, cnext[0] % 4)
-                cnext[0] += 1
+            sfeed.append(("t", 0.225, needs + [("pq", i, b // 2), ("w", "dv")], ("dmm", i, b), f))
+            act.append(("s", 0.447, [("dmm", i, b)] + ([("store", i - 2)] if i >= 2 and b == 0 else []), ("sfree", n), h))
+            if i == TILES - 1 or b == SUB - 1:
+                loads.append(("dma", 0.1, [("sfree", n)], ("store", i), s))
 
-        state = {"ln": None, "o": None, "n": 1, "l": -1}
-        wq = []
+        def gammas():
+            nc.scalar.activation(out=lgam[:], in_=gam[:], func=ACT.Ln)
 
-        def weights_work(n):
-            for _ in range(n):
-                if wq:
-                    fn, ar, kw = wq.pop(0)
-                    fn(*ar, **kw)
+        def constants():
+            nc.vector.tensor_tensor(out=lrho[:], in0=lgam[:, 1, :], in1=lgam[:, 0, :], op=ALU.subtract)
+            nc.vector.tensor_copy(out=gfull[:], in_=gcol[:])
+            nc.vector.tensor_scalar(out=ghalf[:], in0=gcol[:], scalar1=0.5, scalar2=None, op0=ALU.mult)
 
-        def step(i, l, sig=(), wn=0):
-            j = state["ln"]
-            lo = state["o"]
-            n = state["n"] if i is not None else TILES
-            nl = l + 1 if l is not None else (state["l"] + 1)
-            if j is not None:
-                logk(j, 0)
-                logk(j, 1)
+        def copy_scale():
+            nc.vector.tensor_copy(out=scale[:, D:], in_=scale[:, :D])
+
+        table("ln")
+        load_x(0)
+        loads.append(("dma", 0.1, [], ("scale",), load_scale))
+        load_w("s1", ss[1])
+        load_w("s0", ss[0])
+        load_x(1)
+        load_w("c1", cs[1])
+        load_w("c0", cs[0])
+        load_x(2)
+        load_w("dv", dv)
+        load_x(3)
+        weight("s1", "s")
+        widen(0, 0, False)
+        widen(0, 1, False)
+        weight("s0", "v")
+        empty(0, 0)
+        empty(0, 1)
+        weight_quant("s1")
+        weight_quant("s0")
+        quant_x(0)
+        act.append(("s", 0.05, [("scale",)], ("lgam",), gammas))
+        vec.append(("v", 0.25, [("scale",)], ("scale2",), copy_scale))
+        vec.append(("v", 0.15, [("lgam",)], ("lrho",), constants))
+        vec.append(("v", 0.0, [], ("gain",), lambda: None))
+        widen(1, 0, True)
+        widen(1, 1, True)
+
+        todo = []
+        for w in ("c1", "c0", "n0", "dv"):
+            todo.append((weight, (w, "v")))
+            todo.append((weight_quant, (w,)))
+
+        zdue = []
+        lastp, lastt, nx = None, None, 1
+        for i, l, sig, wn in STEPS:
+            if lastp is not None:
+                log(lastp, 0)
+                log(lastp, 1)
+                zdue.append(lastp)
             for x in sig:
-                if x != j:
+                if x != lastp:
                     sigmoid(x)
+            n = nx if i is not None and nx < TILES else None
             if l is not None:
-                cands(4 * l + 2)
+                late = []
                 blend_m(l, 0)
                 blend_m(l, 1)
-                turn2(n, 0)
-                blend_q(l, 0)
-                vgain2(l, 0)
-                cands(4 * l + 3)
+                late.append(blend_q(l, 0))
                 blend_m(l, 2)
-                blend_q(l, 1)
-                vgain2(l, 1)
-                cands(4 * l + 4)
-                empty_x(n, 0) if n < TILES else None
+                if n is not None:
+                    empty(n, 0)
+                late.append(blend_q(l, 1))
                 blend_m(l, 3)
-                turn2(n, 1)
-                blend_q(l, 2)
-                vgain2(l, 2)
-                blend_q(l, 3)
-                vgain2(l, 3)
-                empty_x(n, 1) if n < TILES else None
-            if j is not None and ZPOS == 0:
-                zsub2(j)
-            if j in sig:
-                sigmoid(j)
-            avail[0] += 4 * len(sig)
-            if i is None:
-                cands(4 * nl + 2)
+                late.append(blend_q(l, 2))
+                late.append(blend_q(l, 3))
+                if n is not None:
+                    empty(n, 1)
+                vec.extend([x for x in late if x is not None])
+            elif n is not None:
+                empty(n, 0)
+                if nx + 1 < TILES:
+                    widen(nx + 1, 0, True)
+                empty(n, 1)
+                if nx + 1 < TILES:
+                    widen(nx + 1, 1, True)
+            wide_early = l is None and i is not None and nx + 1 < TILES
+            if lastp is not None and ZL == 0:
+                difference(zdue.pop(0))
+            if lastp in sig:
+                sigmoid(lastp)
             for t in range(4):
                 if i is not None:
                     square(i, 0, t)
                     square(i, 1, t)
-                if l is None and t in (1, 3) and n < TILES:
-                    turn2(n, t // 2)
-                    empty_x(n, t // 2)
-                if i is not None and t == 2:
-                    cands(4 * nl + 2)
-                if lo is not None:
-                    div(lo, t)
-            if i is not None and n < TILES:
+                if lastt is not None:
+                    div(lastt, t)
+            if n is not None:
                 quant_x(n)
-                if i + 4 < TILES:
-                    load_x(i + 4)
+            if i is not None and i + 4 < TILES:
+                load_x(i + 4)
+            for _ in range(wn):
+                if todo:
+                    fn, args = todo.pop(0)
+                    fn(*args)
             if l is not None:
-                flux_h(l, 0)
-            if j is not None and ZPOS == 1:
-                zsub2(j)
-            weights_work(wn)
+                flux(l, 0)
+                flux(l, 1)
+            if i is not None and nx + 1 < TILES and not wide_early:
+                widen(nx + 1, 0, True)
             if l is not None:
-                flux_h(l, 1)
-                quant_ph(l, 0)
-                quant_ph(l, 1)
+                quant_p(l, 0)
+            if i is not None and nx + 1 < TILES and not wide_early:
+                widen(nx + 1, 1, True)
+            if l is not None:
+                quant_p(l, 1)
             if i is not None:
-                widen2(n + 1)
-                state["n"] = n + 1
-            if l is not None:
-                state["l"] = l
-            state["ln"] = i
-            state["o"] = l
-
-        def wprep(name, raw, eng, **kw):
-            w_group(name, wraw[raw], eng, **kw)
-
-        dummy = keep.tile([P, 1], F32, name="dummy")
-        nc.scalar.activation(out=dummy[:], in_=half[:], func=ACT.Ln)
-        wprep("s1", "s1", "s")
-        xw[0] = st.tile([P, SUB * D], BF16, name="xw", bufs=2)
+                nx += 1
+            lastp, lastt = i, l
         for b in range(SUB):
-            nc.vector.tensor_tensor(out=xw[0][:, b * D : (b + 1) * D], in0=xby[0][:, b, :].bitcast(FP8), in1=scale[:, :D], op=ALU.mult)
-            if b == 1:
-                turn2(0, 0)
-        turn2(0, 1)
-        wprep("s0", "s0", "v")
-        empty2(0)
-        w_quant("s1")
-        w_quant("s0")
-        quant_x(0)
-        nc.vector.tensor_copy(out=scale[:, D:], in_=scale[:, :D])
-        constants_s()
-        constants_v()
-        widen2(1)
-        load_w("c0", cs[0], nc.sync)
-        load_x(2)
-        load_w("dv", dv, nc.sync)
-        load_x(3)
-        wq += [
-            (wprep, ("c1", "c1", WE[0]), {}),
-            (w_quant, ("c1",), {}),
-            (wprep, ("c0", "c0", WE[1]), {}),
-            (w_quant, ("c0",), {}),
-            (wprep, ("n0", "c0", WE[2]), {"sign": -1.0}),
-            (w_quant, ("n0",), {}),
-            (wprep, ("dv", "dv", WE[3]), {"permute": False}),
-            (w_quant, ("dv",), {}),
-        ]
-        for what in PROGRAM:
-            step(*what)
-        for b in range(SUB):
-            div(state["o"], b)
+            div(lastt, b)
+        issue([vec, act, gps, sfeed, vfeed, loads], {})

@@ -10,6 +10,7 @@ P = 128
 TOK = 512
 TILES = B // TOK
 SUB = TOK // P
+WORD = 4
 
 F32 = mybir.dt.float32
 BF16 = mybir.dt.bfloat16
@@ -20,470 +21,527 @@ FP8X4 = mybir.dt.float8_e4m3fn_x4
 ALU = mybir.AluOpType
 ACT = mybir.ActivationFunctionType
 
-STEPS = ((0, None, (), 3), (1, None, (), 3), (None, None, (0, 1), 8), (2, 0, (), 0), (3, None, (), 0), (4, 1, (), 0), (None, None, (2, 3, 4), 0), (5, 2, (), 0), (6, 3, (), 0), (None, 4, (5, 6), 0), (7, 5, (), 0), (None, 6, (7,), 0), (None, 7, (), 0))
-SPS = 3
-DPS = 2
-QPS = 2
-XPS = 1
-RUN = 2
-VG = (2, 2, 2, 2, 2, 2, 2, 2)
-EXS = (0,)
-ZL = 0
-WORDER = 0
-LATX = 0.07
-LATP = 0.17
-OV = ()
+STEPS = (
+    (0, None, ()),
+    (1, None, ()),
+    (2, None, ()),
+    (None, None, (0, 1, 2)),
+    (3, 0, ()),
+    (4, 1, ()),
+    (5, 2, ()),
+    (None, None, (3, 4, 5)),
+    (6, 3, ()),
+    (7, 4, ()),
+    (None, 5, (6, 7)),
+    (None, 6, ()),
+    (None, 7, ()),
+)
+S_BANKS = 3
+X_BANKS = 1
+D_BANKS = 2
+Q_BANKS = 2
+OUT_ON_SCALAR = 3
+KEPT = 7
+PIECES = 3
+GAINS_STEP = 1
+RUN = 4
+
+SAME, CROSS, BEHIND_TENSOR = {"vector": 0.18}, 0.07, 0.17
 
 
-def issue(streams, clock):
-    done = {}
-    table = [None]
-    heads = [0] * len(streams)
-    left = sum(len(s) for s in streams)
-    while left:
+def issue(streams):
+    ready = {}
+    clock = {}
+    heads = {name: 0 for name in streams}
+    while True:
         best = None
-        for n, s in enumerate(streams):
-            if heads[n] == len(s):
+        for name in streams:
+            if heads[name] == len(streams[name]):
                 continue
-            engine, cost, needs, gives, fn = s[heads[n]]
-            t = clock.get(engine, 0.0)
-            ok = True
+            engine = name.split(":")[0]
+            cost, needs, gives, write = streams[name][heads[name]]
+            if not all(x in ready for x in needs):
+                continue
+            start = clock.get(engine, 0.0)
             for x in needs:
-                if x not in done:
-                    ok = False
-                    break
-                e, d = done[x]
-                t = max(t, d + (0.18 if e == engine and e == "v" else 0.0 if e == engine else LATP if e == "t" else LATX))
-            if ok and (best is None or t < best[0]):
-                best = (t, n)
-        t, n = best
-        engine, cost, needs, gives, fn = streams[n][heads[n]]
-        fn()
-        heads[n] += 1
-        left -= 1
-        clock[engine] = t + cost
-        if gives is not None:
-            done[gives] = (engine, t + cost)
+                source, end = ready[x]
+                lag = SAME.get(engine, 0.0) if source == engine else BEHIND_TENSOR if source == "tensor" else CROSS
+                start = max(start, end + lag)
+            if best is None or start < best[0]:
+                best = (start, name, engine)
+        if best is None:
+            break
+        start, name, engine = best
+        cost, needs, gives, write = streams[name][heads[name]]
+        write()
+        heads[name] += 1
+        clock[engine] = start + cost
+        ready[gives] = (engine, start + cost)
+    assert all(heads[name] == len(streams[name]) for name in streams)
 
 
 def tile_learnedstencilwenostep_t_kernel(tc, x_bytes, x_scale, cs, ss, gamma, g, dv, out):
     nc = tc.nc
     with ExitStack() as ctx:
         keep = ctx.enter_context(tc.tile_pool(name="keep", bufs=1))
-        wst = ctx.enter_context(tc.tile_pool(name="wst", bufs=2))
-        st = ctx.enter_context(tc.tile_pool(name="st", bufs=2))
+        ring = ctx.enter_context(tc.tile_pool(name="ring", bufs=2))
         psum = ctx.enter_context(tc.psum_pool(name="psum", bufs=1))
         ctx.enter_context(tc.manual_schedule())
 
-        loads, vec, act, gps, sfeed, vfeed = [], [], [], [], [], []
+        streams = {name: [] for name in ("vector", "scalar", "gpsimd", "tensor:scalar", "tensor:vector", "sync")}
+
+        def add(stream, cost, needs, gives, write):
+            streams[stream].append((cost, needs, gives, write))
 
         scale = keep.tile([P, 2 * D], F32, name="scale")
-        gam = keep.tile([P, 2, 4], BF16, name="gam")
-        gcol = keep.tile([P, 4], BF16, name="gcol")
+        scale_col = keep.tile([P, WORD], F32, name="scale_col")
+        gamma_col = keep.tile([P, 2, WORD], BF16, name="gamma_col")
+        g_col = keep.tile([P, WORD], BF16, name="g_col")
+        ln_gamma = keep.tile([P, 2, WORD], F32, name="ln_gamma")
+        ln_ratio = keep.tile([P, WORD], F32, name="ln_ratio")
+        g_full = keep.tile([P, WORD], F32, name="g_full")
+        g_half = keep.tile([P, WORD], F32, name="g_half")
         ident = keep.tile([P, P], F32, name="ident")
         half = keep.tile([P, 1], F32, name="half")
-        dummy = keep.tile([P, 1], F32, name="dummy")
-        lgam = keep.tile([P, 2, 4], F32, name="lgam")
-        lrho = keep.tile([P, 4], F32, name="lrho")
-        gfull = keep.tile([P, 4], F32, name="gfull")
-        ghalf = keep.tile([P, 4], F32, name="ghalf")
+        table = keep.tile([P, 1], F32, name="table")
         make_identity(nc, ident[:])
         nc.vector.memset(half[:], 0.5)
-        nc.scalar.activation(out=dummy[:], in_=half[:], func=ACT.Ln)
-        codes, scales, wraw, wgrp = {}, {}, {}, {}
-        for w in ("s0", "s1", "c1", "c0", "n0", "dv"):
-            codes[w] = keep.tile([P, 512], U32, name="codes_" + w, align_bytes=64)
-            scales[w] = keep.tile([P, 512], U8, name="scales_" + w, align_bytes=64)
-        xby, xw, xps, xg, xc, xs = {}, {}, {}, {}, {}, {}
-        a, qh, vv, dps, qps, sps = {}, {}, {}, {}, {}, {}
-        pg, pc, psc, osb = {}, {}, {}, {}
+        nc.scalar.activation(out=table[:], in_=half[:], func=ACT.Ln)
+
+        codes = {}
+        scales = {}
+        for w in ("s0", "s1", "c0", "c1", "n0", "dv"):
+            codes[w] = keep.tile([P, F], U32, name="codes_" + w, align_bytes=64)
+            scales[w] = keep.tile([P, F], U8, name="scales_" + w, align_bytes=64)
+        x_codes = {}
+        x_scales = {}
+        for i in range(TILES):
+            x_codes[i] = keep.tile([P, TOK], U32, name="x_codes_%d" % i, align_bytes=64)
+            x_scales[i] = keep.tile([P, TOK], U8, name="x_scales_%d" % i, align_bytes=64)
+
+        held = {}
+
+        def part(t):
+            return slice(t * TOK, (t + 1) * TOK)
+
+
+        def take(name, depth, needs_of, key, shape):
+            n = used.get(name, 0)
+            used[name] = n + 1
+
+            def make():
+                held[key] = psum.tile(shape, F32, name=name, bufs=depth)
+                return held[key]
+
+            return n, [(needs_of, n - depth)] if n >= depth else [], make
+
+        used = {}
 
         def load_x(i):
-            def f():
-                xby[i] = st.tile([P, SUB, D], U8, name="xby", bufs=4)
+            def write():
+                held["bytes", i] = ring.tile([P, SUB, D], U8, name="x_raw", bufs=4)
                 rows = x_bytes[i * TOK : (i + 1) * TOK, :]
-                nc.sync.dma_start(out=xby[i][:], in_=rows.rearrange("(p b) k -> p b k", b=SUB))
+                nc.sync.dma_start(out=held["bytes", i][:], in_=rows.rearrange("(p b) k -> p b k", b=SUB))
 
-            loads.append(("dma", 0.5, [("xw", i - 4, 1)] if i >= 4 else [], ("xby", i), f))
+            add("sync", 0.5, [("wide", i - 4, 1)] if i >= 4 else [], ("bytes", i), write)
 
-        def load_w(w, src):
-            def f():
-                wraw[w] = wst.tile([P, 4, 512], BF16, name="wraw", bufs=3)
-                nc.sync.dma_start(out=wraw[w][:], in_=src.rearrange("(p j) c -> p j c", j=4))
+        def load_weight(w, source, reader):
+            def write():
+                held["raw", w] = ring.tile([P, WORD, F], BF16, name="w_raw", bufs=3)
+                nc.sync.dma_start(out=held["raw", w][:], in_=source.rearrange("(p j) c -> p j c", j=WORD))
 
-            k = len(wq)
-            loads.append(("dma", 1.0, [("wg", wq[k - 3])] if k >= 3 else [], ("wraw", w), f))
-            wq.append(w)
-
-        wq = []
+            add("sync", 1.0, [("grouped", reader)] if reader else [], ("raw", w), write)
 
         def load_scale():
-            nc.scalar.dma_start(out=scale[:, :D], in_=x_scale.rearrange("o k -> (o k)").partition_broadcast(P))
-            nc.scalar.dma_start(out=gam[:], in_=gamma.rearrange("k (p t) -> p k t", t=4))
-            nc.scalar.dma_start(out=gcol[:], in_=g.rearrange("(p t) -> p t", t=4))
+            nc.sync.dma_start(out=scale_col[:], in_=x_scale.rearrange("o (p t) -> p (o t)", t=WORD))
 
-        def weight(w, engine):
-            def group():
-                wgrp[w] = wst.tile([P, 2048], BF16, name="wgrp", bufs=3, align_bytes=64)
+        def load_gains():
+            nc.sync.dma_start(out=gamma_col[:], in_=gamma.rearrange("k (p t) -> p k t", t=WORD))
+            nc.sync.dma_start(out=g_col[:], in_=g.rearrange("(p t) -> p t", t=WORD))
+
+        def spread_scale():
+            n, needs, make = take("s_bank", S_BANKS, "s_read", "spread", [P, WORD, P])
+
+            def turn():
+                bank = make()
+                for t in range(WORD):
+                    nc.tensor.transpose(bank[:, t, :], scale_col[:, t : t + 1].to_broadcast([P, P]), ident[:])
+
+            def copy():
+                bank = held["spread"]
+                nc.scalar.copy(out=scale[:, :D].rearrange("p (n t) -> p n t", t=WORD), in_=bank[:].rearrange("p t n -> p n t"))
+
+            def double():
+                nc.vector.tensor_copy(out=scale[:, D:], in_=scale[:, :D])
+
+            add("tensor:scalar", 0.5, needs + [("scale_col",)], ("spread",), turn)
+            add("scalar", 0.45, [("spread",)], ("s_read", n), copy)
+            return double
+
+        def log_gammas():
+            nc.scalar.activation(out=ln_gamma[:], in_=gamma_col[:], func=ACT.Ln)
+
+        def gains():
+            nc.vector.tensor_tensor(out=ln_ratio[:], in0=ln_gamma[:, 1, :], in1=ln_gamma[:, 0, :], op=ALU.subtract)
+            nc.vector.tensor_copy(out=g_full[:], in_=g_col[:])
+            nc.vector.tensor_scalar(out=g_half[:], in0=g_col[:], scalar1=0.5, scalar2=None, op0=ALU.mult)
+
+        def group_weight(w, engine):
+            def write():
+                grouped = ring.tile([P, WORD * F], BF16, name="w_grouped", bufs=3, align_bytes=64)
+                held["grouped", w] = grouped
                 if w == "n0":
-                    nc.vector.tensor_scalar(out=wgrp[w][:], in0=wgrp["c0"][:], scalar1=-1.0, scalar2=None, op0=ALU.mult)
+                    nc.vector.tensor_scalar(
+                        out=grouped[:], in0=held["grouped", "c0"][:], scalar1=-1.0, scalar2=None, op0=ALU.mult
+                    )
                     return
+                raw = held["raw", w]
                 if w == "dv":
-                    o = wgrp[w][:].rearrange("p (c j) -> p c j", j=4)
-                    i = wraw[w][:].rearrange("p j c -> p c j")
+                    dst = grouped[:].rearrange("p (c j) -> p c j", j=WORD)
+                    src = raw[:].rearrange("p j c -> p c j")
                 else:
-                    o = wgrp[w][:].rearrange("p (t m j) -> p t m j", t=4, j=4)
-                    i = wraw[w][:].rearrange("p j (m t) -> p t m j", t=4)
-                if engine == "v":
-                    nc.vector.tensor_copy(out=o, in_=i)
+                    dst = grouped[:].rearrange("p (t m j) -> p t m j", t=WORD, j=WORD)
+                    src = raw[:].rearrange("p j (m t) -> p t m j", t=WORD)
+                if engine == "vector":
+                    nc.vector.tensor_copy(out=dst, in_=src)
                 else:
-                    nc.scalar.copy(out=o, in_=i)
+                    nc.scalar.copy(out=dst, in_=src)
 
-            cost = 0.46 if w == "n0" else 1.07 if engine == "v" else 2.0
-            need = ("wg", "c0") if w == "n0" else ("wraw", w)
-            (vec if engine == "v" else act).append((engine, cost, [need], ("wg", w), group))
+            cost = 0.46 if w == "n0" else 1.07 if engine == "vector" else 2.0
+            add(engine, cost, [("grouped", "c0") if w == "n0" else ("raw", w)], ("grouped", w), write)
 
-        def weight_quant(w):
-            def f():
-                nc.vector.quantize_mx(out=codes[w][:].bitcast(FP8X4), scales=scales[w][:], in_=wgrp[w][:])
+        def quantise_weight(w):
+            def write():
+                nc.vector.quantize_mx(out=codes[w][:].bitcast(FP8X4), scales=scales[w][:], in_=held["grouped", w][:])
 
-            vec.append(("v", 0.48, [("wg", w)], ("w", w), f))
+            add("vector", 0.48, [("grouped", w)], ("weight", w), write)
 
-        def widen(i, h, wide):
-            def f():
+        def widen(i, h, width):
+            def write():
                 if h == 0:
-                    xw[i] = st.tile([P, SUB * D], BF16, name="xw", bufs=2)
-                src = xby[i][:].rearrange("p b k -> p (b k)")
-                n = 2 * D if wide else D
-                for c in range(h * 2 * D, (h + 1) * 2 * D, n):
+                    held["wide", i] = ring.tile([P, SUB * D], BF16, name="x_wide", bufs=2)
+                src = held["bytes", i][:].rearrange("p b k -> p (b k)")
+                for c in range(2 * D * h, 2 * D * (h + 1), width):
                     nc.vector.tensor_tensor(
-                        out=xw[i][:, c : c + n], in0=src[:, c : c + n].bitcast(FP8), in1=scale[:, :n], op=ALU.mult
+                        out=held["wide", i][:, c : c + width],
+                        in0=src[:, c : c + width].bitcast(FP8),
+                        in1=scale[:, :width],
+                        op=ALU.mult,
                     )
 
-            needs = [("xby", i)] + ([("turn", i - 2, 1)] if i >= 2 else []) + ([("scale2",)] if wide else [("scale",)])
-            vec.append(("v", 0.88 if wide else 0.91, needs, ("xw", i, h), f))
+            needs = [("bytes", i), ("s_read", 0) if width == D else ("scale",)]
+            add("vector", 0.9, needs + ([("turned", i - 2, 1)] if i >= 2 else []), ("wide", i, h), write)
 
-        def turn(i, h):
-            def f():
-                xps[i, h] = psum.tile([P, 2, 2, P], F32, name="xps", bufs=XPS)
-                for b in (0, 1):
-                    c0 = (2 * h + b) * D
-                    words = xw[i][:, c0 : c0 + D].bitcast(F32)
+        def turn(i, h, reader):
+            n, needs, make = take("x_bank", X_BANKS, "x_read", ("turned", i, h), [P, 2, 2, P])
+
+            def turn_words():
+                bank = make()
+                for b in range(2):
+                    words = held["wide", i][:, (2 * h + b) * D : (2 * h + b + 1) * D].bitcast(F32)
                     for u in range(2):
-                        nc.tensor.transpose(xps[i, h][:, b, u, :], words[:, u : D // 2 : 2], ident[:])
+                        nc.tensor.transpose(bank[:, b, u, :], words[:, u : D // 2 : 2], ident[:])
 
-            k = 2 * i + h - XPS
-            vfeed.append(("t", 0.45, [("xw", i, h)] + ([("xg", k // 2, k % 2)] if k >= 0 else []), ("turn", i, h), f))
-
-        def empty(i, h):
-            def f():
+            def empty():
                 if h == 0:
-                    xg[i] = st.tile([P, TOK * 4], BF16, name="xg", bufs=2, align_bytes=64)
-                o = xg[i][:, h * 1024 : (h + 1) * 1024].bitcast(F32).rearrange("p (b n u) -> p b n u", b=2, u=2)
-                src = xps[i, h][:].rearrange("p b u n -> p b n u")
-                if i in EXS:
-                    nc.scalar.copy(out=o, in_=src)
+                    held["x_grouped", i] = ring.tile([P, TOK * WORD], BF16, name="x_grouped", bufs=2, align_bytes=64)
+                dst = held["x_grouped", i][:, 1024 * h : 1024 * (h + 1)].bitcast(F32)
+                dst = dst.rearrange("p (b n u) -> p b n u", b=2, u=2)
+                src = held["turned", i, h][:].rearrange("p b u n -> p b n u")
+                if reader == "scalar":
+                    nc.scalar.copy(out=dst, in_=src)
                 else:
-                    nc.vector.tensor_copy(out=o, in_=src)
+                    nc.vector.tensor_copy(out=dst, in_=src)
 
-            turn(i, h)
-            e = "s" if i in EXS else "v"
-            (act if i in EXS else vec).append((e, 0.455, [("turn", i, h)] + ([("xq", i - 2)] if i >= 2 else []), ("xg", i, h), f))
+            add("tensor:vector", 0.45, needs + [("wide", i, h)], ("turned", i, h), turn_words)
+            add(reader, 0.455, [("turned", i, h)] + ([("x", i - 2)] if i >= 2 else []), ("x_read", n), empty)
+            return n
 
-        def quant_x(i):
-            def f():
-                xc[i] = keep.tile([P, TOK], U32, name="xc%d" % i, align_bytes=64)
-                xs[i] = keep.tile([P, TOK], U8, name="xs%d" % i, align_bytes=64)
-                nc.vector.quantize_mx(out=xc[i][:].bitcast(FP8X4), scales=xs[i][:], in_=xg[i][:])
+        def quantise_x(i, banks):
+            def write():
+                nc.vector.quantize_mx(
+                    out=x_codes[i][:].bitcast(FP8X4), scales=x_scales[i][:], in_=held["x_grouped", i][:]
+                )
 
-            vec.append(("v", 0.48, [("xg", i, 0), ("xg", i, 1)], ("xq", i), f))
+            add("vector", 0.48, [("x_read", n) for n in banks], ("x", i), write)
 
-        def mm(ps, w, t, i, start, stop):
+        def stage1(bank, w, t, i, start, stop):
             nc.tensor.matmul_mx(
-                out=ps[:],
-                lhsT=codes[w][:, t * P : (t + 1) * P].bitcast(FP8X4),
-                lhsT_scale=scales[w][:, t * P : (t + 1) * P],
-                rhs=xc[i][:].bitcast(FP8X4),
-                rhs_scale=xs[i][:],
+                out=bank[:],
+                lhsT=codes[w][:, P * t : P * (t + 1)].bitcast(FP8X4),
+                lhsT_scale=scales[w][:, P * t : P * (t + 1)],
+                rhs=x_codes[i][:].bitcast(FP8X4),
+                rhs_scale=x_scales[i][:],
                 start=start,
                 stop=stop,
             )
 
-        ring = []
-
-        def ring_needs():
-            n = len(ring)
-            ring.append(n)
-            return n, ([("sfree", n - SPS)] if n >= SPS else [])
-
-        arel = {}
-
         def square(i, k, t):
-            n, needs = ring_needs()
+            n, needs, make = take("s_bank", S_BANKS, "s_read", ("s_bank", i, k, t), [P, TOK])
 
-            def f():
-                sps[n] = psum.tile([P, TOK], F32, name="sps", bufs=SPS)
-                mm(sps[n], "s%d" % k, t, i, True, True)
+            def multiply():
+                stage1(make(), "s%d" % k, t, i, True, True)
 
-            def h():
+            def write():
                 if t == 0:
-                    a[i, k] = st.tile([P, 4 * TOK], F32, name="a%d" % k, bufs=7 if k == 0 else 2)
-                nc.scalar.activation(out=a[i, k][:, t * TOK : (t + 1) * TOK], in_=sps[n][:], func=ACT.Square)
+                    held["s", i, k] = ring.tile([P, WORD * TOK], F32, name="s%d" % k, bufs=KEPT if k == 0 else 2)
+                bank = held["s_bank", i, k, t]
+                nc.scalar.activation(out=held["s", i, k][:, part(t)], in_=bank[:], func=ACT.Square)
 
-            sfeed.append(("t", 0.225, needs + [("xq", i), ("w", "s%d" % k)], ("smm", n), f))
-            more = []
+            free = []
+            if t == 0 and k == 0 and i >= KEPT:
+                free = [("d_read", WORD * (i - KEPT) + WORD - 1)]
             if t == 0 and k == 1 and i >= 2:
-                more = [("z", i - 2)]
-            if t == 0 and k == 0 and i >= 7:
-                more = [("m", i - 7, 3)]
-            act.append(("s", 0.447, [("smm", n)] + more, ("sfree", n), h))
+                free = [("z", i - 2)]
+            add("tensor:scalar", 0.225, needs + [("x", i), ("weight", "s%d" % k)], ("s_bank", n), multiply)
+            add("scalar", 0.45, [("s_bank", n)] + free, ("s_read", n), write)
 
-        mode = [None]
+        def table_load(func):
+            change = 0.0 if current[0] == func else 1.3
+            current[0] = func
+            return change
 
-        def table(m):
-            c = 0.0 if mode[0] == m else 1.3
-            mode[0] = m
-            return c
+        current = [ACT.Ln]
 
-        def log(i, k):
-            def f():
-                z = a[i, k][:]
-                nc.scalar.activation(out=z, in_=z, func=ACT.Ln, bias=half[:, 0:1])
+        def logarithm(i, k):
+            def write():
+                s = held["s", i, k]
+                nc.scalar.activation(out=s[:], in_=s[:], func=ACT.Ln, bias=half[:, 0:1])
 
-            act.append(("s", 1.73 + table("ln"), [], ("ln", i, k), f))
+            add("scalar", 1.73 + table_load(ACT.Ln), [], ("ln", i, k), write)
 
         def difference(i):
-            def f():
-                nc.vector.tensor_tensor(out=a[i, 0][:], in0=a[i, 0][:], in1=a[i, 1][:], op=ALU.subtract)
-
-            vec.append(("v", 1.73, [("ln", i, 1)], ("z", i), f))
-
-        def sigmoid(i):
-            for t in range(4):
-
-                def f(t=t):
-                    z = a[i, 0][:, t * TOK : (t + 1) * TOK]
-                    nc.scalar.activation(out=z, in_=z, func=ACT.Sigmoid, bias=lrho[:, t : t + 1], scale=2.0)
-
-                act.append(("s", 0.447 + table("sig"), [("z", i), ("lrho",)], ("sig", i, t), f))
-
-        def cand(i, t):
-            n = 4 * i + t
-
-            def fd():
-                dps[n] = psum.tile([P, TOK], F32, name="dps", bufs=DPS)
-                mm(dps[n], "c1", t, i, True, False)
-                mm(dps[n], "n0", t, i, False, True)
-
-            def fq():
-                qps[n] = psum.tile([P, TOK], F32, name="qps", bufs=QPS)
-                mm(qps[n], "c0", t, i, True, True)
-
-            kd, kq = n - DPS, n - QPS
-            vfeed.append(("t", 0.45, [("w", "n0"), ("w", "c1"), ("xq", i)] + ([("m", kd // 4, kd % 4)] if kd >= 0 else []), ("d", i, t), fd))
-            vfeed.append(("t", 0.225, [("w", "c0"), ("xq", i)] + ([("q", kq // 4, kq % 4)] if kq >= 0 else []), ("qp", i, t), fq))
-
-        def blend_m(i, t):
-            def f():
-                if t == 0:
-                    qh[i] = st.tile([P, 4 * TOK], F32, name="qh", bufs=2)
-                s_ = slice(t * TOK, (t + 1) * TOK)
-                nc.vector.tensor_tensor(out=qh[i][:, s_], in0=a[i, 0][:, s_], in1=dps[4 * i + t][:], op=ALU.mult)
-
-            cand(i, t)
-            vec.append(("v", 0.455, [("d", i, t), ("sig", i, t)], ("m", i, t), f))
-
-        def blend_q(i, t):
-            def f():
-                s_ = slice(t * TOK, (t + 1) * TOK)
-                nc.vector.tensor_tensor(out=qh[i][:, s_], in0=qh[i][:, s_], in1=qps[4 * i + t][:], op=ALU.add)
-
-            def v():
-                if t == 0:
-                    vv[i] = st.tile([P, 4 * TOK], F32, name="vv", bufs=2)
-                s_ = slice(t * TOK, (t + 1) * TOK)
-                e = VG[i]
-                if e == 1:
-                    nc.scalar.activation(out=vv[i][:, s_], in_=qh[i][:, s_], func=ACT.Identity, scale=ghalf[:, t : t + 1], bias=gfull[:, t : t + 1])
-                else:
-                    eng = nc.gpsimd if e == 2 else nc.vector
-                    eng.tensor_scalar(
-                        out=vv[i][:, s_], in0=qh[i][:, s_], scalar1=ghalf[:, t : t + 1], scalar2=gfull[:, t : t + 1], op0=ALU.mult, op1=ALU.add
-                    )
-
-            vec.append(("v", 0.455, [("qp", i, t), ("m", i, t)], ("q", i, t), f))
-            e = "vsg"[VG[i]]
-            late = (e, {"v": 0.24, "s": 0.447, "g": 0.55}[e], [("q", i, t), ("gain",)] + ([("pg", i - 2, 1)] if i >= 2 else []), ("v", i, t), v)
-            if e == "v":
-                return late
-            (gps if e == "g" else act).append(late)
-            return None
-
-        def flux(i, h):
-            def f():
-                if h == 0:
-                    pg[i] = st.tile([P, TOK * 4], BF16, name="pg", bufs=2, align_bytes=64)
-                o = pg[i][:, h * 1024 : (h + 1) * 1024].rearrange("p (c i t) -> p c t i", i=RUN, t=4)
-                q_ = qh[i][:].rearrange("p (t h c i) -> p h c t i", t=4, i=RUN, h=2)[:, h]
-                v_ = vv[i][:].rearrange("p (t h c i) -> p h c t i", t=4, i=RUN, h=2)[:, h]
-                nc.vector.tensor_tensor(out=o, in0=q_, in1=v_, op=ALU.mult)
-
-            vec.append(("v", 0.88, [("v", i, t) for t in range(4)], ("pg", i, h), f))
-
-        def quant_p(i, h):
-            def f():
-                if h == 0:
-                    pc[i] = st.tile([P, TOK], U32, name="pc", bufs=2, align_bytes=64)
-                    psc[i] = st.tile([P, TOK], U8, name="psc", bufs=2, align_bytes=64)
-                s_ = slice(h * 256, (h + 1) * 256)
-                nc.vector.quantize_mx(
-                    out=pc[i][:, s_].bitcast(FP8X4), scales=psc[i][:, s_], in_=pg[i][:, h * 1024 : (h + 1) * 1024]
+            def write():
+                nc.vector.tensor_tensor(
+                    out=held["s", i, 0][:], in0=held["s", i, 0][:], in1=held["s", i, 1][:], op=ALU.subtract
                 )
 
-            vec.append(("v", 0.26, [("pg", i, h)] + ([("dmm", i - 2, 3)] if i >= 2 else []), ("pq", i, h), f))
+            add("vector", 1.73, [("ln", i, 1)], ("z", i), write)
 
-        def div(i, b):
-            n, needs = ring_needs()
+        def sigmoid(i):
+            for t in range(WORD):
 
-            def f():
-                sps[n] = psum.tile([P, D], F32, name="sps", bufs=SPS)
+                def write(t=t):
+                    z = held["s", i, 0][:, part(t)]
+                    nc.scalar.activation(out=z, in_=z, func=ACT.Sigmoid, bias=ln_ratio[:, t : t + 1], scale=2.0)
+
+                add("scalar", 0.45 + table_load(ACT.Sigmoid), [("z", i), ("gains",)], ("weighted", i, t), write)
+
+        def blend_m(i, t):
+            n, needs, make = take("d_bank", D_BANKS, "d_read", ("d_bank", i, t), [P, TOK])
+            nq, needs_q, make_q = take("q_bank", Q_BANKS, "q_read", ("q_bank", i, t), [P, TOK])
+
+            def multiply_d():
+                bank = make()
+                stage1(bank, "c1", t, i, True, False)
+                stage1(bank, "n0", t, i, False, True)
+
+            def multiply_q():
+                stage1(make_q(), "c0", t, i, True, True)
+
+            def write():
+                if t == 0:
+                    held["q", i] = ring.tile([P, WORD * TOK], F32, name="q", bufs=2)
+                bank = held["d_bank", i, t]
+                nc.vector.tensor_tensor(
+                    out=held["q", i][:, part(t)], in0=held["s", i, 0][:, part(t)], in1=bank[:], op=ALU.mult
+                )
+
+            weights = [("weight", "c1"), ("weight", "n0")]
+            add("tensor:vector", 0.45, needs + weights + [("x", i)], ("d_bank", n), multiply_d)
+            add("tensor:vector", 0.225, needs_q + [("weight", "c0"), ("x", i)], ("q_bank", nq), multiply_q)
+            add("vector", 0.455, [("d_bank", n), ("weighted", i, t)], ("d_read", n), write)
+            return nq
+
+        def blend_q(i, t, nq):
+            def write():
+                q = held["q", i][:, part(t)]
+                bank = held["q_bank", i, t]
+                nc.vector.tensor_tensor(out=q, in0=q, in1=bank[:], op=ALU.add)
+
+            def gain():
+                if t == 0:
+                    held["gain", i] = ring.tile([P, WORD * TOK], F32, name="gain", bufs=2)
+                nc.gpsimd.tensor_scalar(
+                    out=held["gain", i][:, part(t)],
+                    in0=held["q", i][:, part(t)],
+                    scalar1=g_half[:, t : t + 1],
+                    scalar2=g_full[:, t : t + 1],
+                    op0=ALU.mult,
+                    op1=ALU.add,
+                )
+
+            add("vector", 0.455, [("q_bank", nq)], ("q_read", nq), write)
+            free = [("pg", i - 2, 1)] if i >= 2 else []
+            add("gpsimd", 0.55, [("q_read", nq), ("gains",)] + free, ("gain", i, t), gain)
+
+        def flux(i, h):
+            def write():
+                if h == 0:
+                    held["pg", i] = ring.tile([P, TOK * WORD], BF16, name="pg", bufs=2, align_bytes=64)
+                dst = held["pg", i][:, 1024 * h : 1024 * (h + 1)]
+                q, gain = (
+                    held[name, i][:].rearrange("p (t h c r) -> p h c t r", t=WORD, h=2, r=RUN)[:, h] for name in ("q", "gain")
+                )
+                nc.vector.tensor_tensor(
+                    out=dst.rearrange("p (c r t) -> p c t r", r=RUN, t=WORD), in0=q, in1=gain, op=ALU.mult
+                )
+
+            add("vector", 0.88, [("gain", i, t) for t in range(WORD)], ("pg", i, h), write)
+
+        def quantise_pg(i, h):
+            def write():
+                if h == 0:
+                    held["pg_codes", i] = ring.tile([P, TOK], U32, name="pg_codes", bufs=2, align_bytes=64)
+                    held["pg_scales", i] = ring.tile([P, TOK], U8, name="pg_scales", bufs=2, align_bytes=64)
+                    held["out", i] = ring.tile([P, SUB, D], F32, name="out_tile", bufs=2)
+                cols = slice(256 * h, 256 * (h + 1))
+                nc.vector.quantize_mx(
+                    out=held["pg_codes", i][:, cols].bitcast(FP8X4),
+                    scales=held["pg_scales", i][:, cols],
+                    in_=held["pg", i][:, 1024 * h : 1024 * (h + 1)],
+                )
+
+            free = [("product", i - 2, SUB - 1), ("stored", i - 2)] if i >= 2 else []
+            add("vector", 0.26, [("pg", i, h)] + free, ("pg_quantised", i, h), write)
+
+        def divergence(i, b):
+            reader = "scalar" if b < OUT_ON_SCALAR else "vector"
+            name, depth = ("s", S_BANKS) if reader == "scalar" else ("x", X_BANKS)
+            n, needs, make = take(name + "_bank", depth, name + "_read", ("product", i, b), [P, D])
+
+            def multiply():
+                bank = make()
                 nc.tensor.matmul_mx(
-                    out=sps[n][:],
-                    lhsT=pc[i][:, b * P : (b + 1) * P].bitcast(FP8X4),
-                    lhsT_scale=psc[i][:, b * P : (b + 1) * P],
+                    out=bank[:],
+                    lhsT=held["pg_codes", i][:, P * b : P * (b + 1)].bitcast(FP8X4),
+                    lhsT_scale=held["pg_scales", i][:, P * b : P * (b + 1)],
                     rhs=codes["dv"][:].bitcast(FP8X4),
                     rhs_scale=scales["dv"][:],
                     start=True,
                     stop=True,
                 )
 
-            def h():
-                if b == 0:
-                    osb[i] = st.tile([P, SUB, D], F32, name="osb", bufs=2)
-                nc.scalar.copy(out=osb[i][:, b, :], in_=sps[n][:])
+            def empty():
+                dst = held["out", i][:, b, :]
+                bank = held["product", i, b]
+                if reader == "scalar":
+                    nc.scalar.copy(out=dst, in_=bank[:])
+                else:
+                    nc.vector.tensor_copy(out=dst, in_=bank[:])
 
             rows = out[i * TOK : (i + 1) * TOK, :].rearrange("(p b) d -> p b d", b=SUB)
 
-            def s():
-                if i == TILES - 1:
-                    nc.sync.dma_start(out=rows[:, b, :], in_=osb[i][:, b, :])
-                else:
-                    nc.sync.dma_start(out=rows, in_=osb[i][:])
+            def store():
+                nc.sync.dma_start(out=rows, in_=held["out", i][:])
 
-            sfeed.append(("t", 0.225, needs + [("pq", i, b // 2), ("w", "dv")], ("dmm", i, b), f))
-            act.append(("s", 0.447, [("dmm", i, b)] + ([("store", i - 2)] if i >= 2 and b == 0 else []), ("sfree", n), h))
-            if i == TILES - 1 or b == SUB - 1:
-                loads.append(("dma", 0.1, [("sfree", n)], ("store", i), s))
+            def store_part():
+                nc.sync.dma_start(out=rows[:, b, :], in_=held["out", i][:, b, :])
 
-        def gammas():
-            nc.scalar.activation(out=lgam[:], in_=gam[:], func=ACT.Ln)
+            add("tensor:" + reader, 0.225, needs + [("pg_quantised", i, b // 2), ("weight", "dv")], ("product", i, b), multiply)
+            add(reader, 0.45, [("product", i, b)], (name + "_read", n), empty)
+            copied[i, b] = (name + "_read", n)
+            if i == TILES - 1:
+                add("sync", 0.1, [copied[i, b]], ("stored", i, b), store_part)
+            elif b == SUB - 1:
+                add("sync", 0.1, [copied[i, x] for x in range(SUB)], ("stored", i), store)
 
-        def constants():
-            nc.vector.tensor_tensor(out=lrho[:], in0=lgam[:, 1, :], in1=lgam[:, 0, :], op=ALU.subtract)
-            nc.vector.tensor_copy(out=gfull[:], in_=gcol[:])
-            nc.vector.tensor_scalar(out=ghalf[:], in0=gcol[:], scalar1=0.5, scalar2=None, op0=ALU.mult)
+        copied = {}
 
-        def copy_scale():
-            nc.vector.tensor_copy(out=scale[:, D:], in_=scale[:, :D])
-
-        table("ln")
+        add("sync", 0.1, [], ("scale_col",), load_scale)
         load_x(0)
-        loads.append(("dma", 0.1, [], ("scale",), load_scale))
-        load_w("s1", ss[1])
-        load_w("s0", ss[0])
+        load_weight("s1", ss[1], None)
+        load_weight("s0", ss[0], None)
         load_x(1)
-        load_w("c1", cs[1])
-        load_w("c0", cs[0])
+        load_weight("c1", cs[1], None)
+        add("sync", 0.1, [], ("gain_cols",), load_gains)
+        load_weight("c0", cs[0], "s1")
         load_x(2)
-        load_w("dv", dv)
+        load_weight("dv", dv, "s0")
         load_x(3)
-        weight("s1", "s")
-        widen(0, 0, False)
-        widen(0, 1, False)
-        weight("s0", "v")
-        empty(0, 0)
-        empty(0, 1)
-        weight_quant("s1")
-        weight_quant("s0")
-        quant_x(0)
-        act.append(("s", 0.05, [("scale",)], ("lgam",), gammas))
-        vec.append(("v", 0.25, [("scale",)], ("scale2",), copy_scale))
-        vec.append(("v", 0.15, [("lgam",)], ("lrho",), constants))
-        vec.append(("v", 0.0, [], ("gain",), lambda: None))
-        widen(1, 0, True)
-        widen(1, 1, True)
+        double_scale = spread_scale()
+        group_weight("s1", "scalar")
+        widen(0, 0, D)
+        widen(0, 1, D)
+        group_weight("s0", "vector")
+        banks = [turn(0, h, "scalar") for h in range(2)]
+        quantise_weight("s1")
+        quantise_weight("s0")
+        quantise_x(0, banks)
+        add("vector", 0.25, [("s_read", 0)], ("scale",), double_scale)
+        widen(1, 0, 2 * D)
+        widen(1, 1, 2 * D)
 
-        todo = []
+        pieces = []
         for w in ("c1", "c0", "n0", "dv"):
-            todo.append((weight, (w, "v")))
-            todo.append((weight_quant, (w,)))
+            pieces.append((group_weight, (w, "vector")))
+            pieces.append((quantise_weight, (w,)))
 
-        zdue = []
-        lastp, lastt, nx = None, None, 1
-        for i, l, sig, wn in STEPS:
-            if lastp is not None:
-                log(lastp, 0)
-                log(lastp, 1)
-                zdue.append(lastp)
-            for x in sig:
-                if x != lastp:
+        last_s = None
+        last_c = None
+        for i, c, sigmoids in STEPS:
+            n = i + 1 if i is not None and i + 1 < TILES else None
+            wider = n + 1 if n is not None and n + 1 < TILES else None
+            if last_s is not None:
+                logarithm(last_s, 0)
+                logarithm(last_s, 1)
+            for x in sigmoids:
+                if x != last_s:
                     sigmoid(x)
-            n = nx if i is not None and nx < TILES else None
-            if l is not None:
-                late = []
-                blend_m(l, 0)
-                blend_m(l, 1)
-                late.append(blend_q(l, 0))
-                blend_m(l, 2)
+
+            banks = []
+            if c is not None:
+                q_banks = [blend_m(c, 0), blend_m(c, 1)]
+                blend_q(c, 0, q_banks[0])
+                q_banks.append(blend_m(c, 2))
                 if n is not None:
-                    empty(n, 0)
-                late.append(blend_q(l, 1))
-                blend_m(l, 3)
-                late.append(blend_q(l, 2))
-                late.append(blend_q(l, 3))
+                    banks.append(turn(n, 0, "vector"))
+                blend_q(c, 1, q_banks[1])
+                q_banks.append(blend_m(c, 3))
+                blend_q(c, 2, q_banks[2])
+                blend_q(c, 3, q_banks[3])
                 if n is not None:
-                    empty(n, 1)
-                vec.extend([x for x in late if x is not None])
+                    banks.append(turn(n, 1, "vector"))
             elif n is not None:
-                empty(n, 0)
-                if nx + 1 < TILES:
-                    widen(nx + 1, 0, True)
-                empty(n, 1)
-                if nx + 1 < TILES:
-                    widen(nx + 1, 1, True)
-            wide_early = l is None and i is not None and nx + 1 < TILES
-            if lastp is not None and ZL == 0:
-                difference(zdue.pop(0))
-            if lastp in sig:
-                sigmoid(lastp)
-            for t in range(4):
+                for h in range(2):
+                    banks.append(turn(n, h, "vector"))
+                    if wider is not None:
+                        widen(wider, h, 2 * D)
+            if last_s is not None:
+                difference(last_s)
+            if last_s in sigmoids:
+                sigmoid(last_s)
+
+            if i == GAINS_STEP:
+                add("scalar", 0.05, [("gain_cols",)], ("ln_gamma",), log_gammas)
+                add("vector", 0.15, [("ln_gamma",)], ("gains",), gains)
+
+            for t in range(WORD):
                 if i is not None:
                     square(i, 0, t)
                     square(i, 1, t)
-                if lastt is not None:
-                    div(lastt, t)
+                if last_c is not None and t < OUT_ON_SCALAR:
+                    divergence(last_c, t)
+            if last_c is not None:
+                for b in range(OUT_ON_SCALAR, SUB):
+                    divergence(last_c, b)
             if n is not None:
-                quant_x(n)
+                quantise_x(n, banks)
             if i is not None and i + 4 < TILES:
                 load_x(i + 4)
-            for _ in range(wn):
-                if todo:
-                    fn, args = todo.pop(0)
-                    fn(*args)
-            if l is not None:
-                flux(l, 0)
-                flux(l, 1)
-            if i is not None and nx + 1 < TILES and not wide_early:
-                widen(nx + 1, 0, True)
-            if l is not None:
-                quant_p(l, 0)
-            if i is not None and nx + 1 < TILES and not wide_early:
-                widen(nx + 1, 1, True)
-            if l is not None:
-                quant_p(l, 1)
-            if i is not None:
-                nx += 1
-            lastp, lastt = i, l
+            for run, args in pieces[:PIECES]:
+                run(*args)
+            pieces = pieces[PIECES:]
+            if c is not None:
+                flux(c, 0)
+                flux(c, 1)
+                if wider is not None:
+                    widen(wider, 0, 2 * D)
+                quantise_pg(c, 0)
+                if wider is not None:
+                    widen(wider, 1, 2 * D)
+                quantise_pg(c, 1)
+            last_s, last_c = i, c
         for b in range(SUB):
-            div(lastt, b)
-        issue([vec, act, gps, sfeed, vfeed, loads], {})
+            divergence(last_c, b)
+        issue(streams)

@@ -7,10 +7,10 @@ B, D, F = 4096, 512, 512
 FLOPS = 5 * 2 * B * D * F
 
 P = 128
+WORD = 4
 TOK = 512
 TILES = B // TOK
 SUB = TOK // P
-WORD = 4
 
 F32 = mybir.dt.float32
 BF16 = mybir.dt.bfloat16
@@ -27,57 +27,50 @@ STEPS = (
     (2, None, ()),
     (None, None, (0, 1, 2)),
     (3, 0, ()),
-    (4, 1, ()),
-    (5, 2, ()),
-    (None, None, (3, 4, 5)),
+    (4, None, ()),
+    (5, 1, ()),
+    (None, 2, (3, 4, 5)),
     (6, 3, ()),
     (7, 4, ()),
     (None, 5, (6, 7)),
     (None, 6, ()),
     (None, 7, ()),
 )
-S_BANKS = 3
-X_BANKS = 1
-D_BANKS = 2
-Q_BANKS = 2
-OUT_ON_SCALAR = 3
-KEPT = 7
-PIECES = 3
-GAINS_STEP = 1
+HELD = 7
+BANKS = {"for_scalar": 3, "for_vector": 1, "difference": 2, "q0": 2}
+OUT_ON_VECTOR = 2
 RUN = 4
 
-SAME, CROSS, BEHIND_TENSOR = {"vector": 0.18}, 0.07, 0.17
+MATMUL = 0.5
+TABLE = 3.0
+REACH = {"vector": 0.5, "scalar": 0.5, "gpsimd": 0.5, "sync": 0.5, "tensor": 2.0}
 
 
 def issue(streams):
-    ready = {}
-    clock = {}
-    heads = {name: 0 for name in streams}
-    while True:
-        best = None
+    given = {}
+    free = {}
+    position = {name: 0 for name in streams}
+    while any(position[name] < len(streams[name]) for name in streams):
+        first = None
         for name in streams:
-            if heads[name] == len(streams[name]):
+            if position[name] == len(streams[name]):
                 continue
             engine = name.split(":")[0]
-            cost, needs, gives, write = streams[name][heads[name]]
-            if not all(x in ready for x in needs):
+            needs = streams[name][position[name]][1]
+            if not all(x in given for x in needs):
                 continue
-            start = clock.get(engine, 0.0)
-            for x in needs:
-                source, end = ready[x]
-                lag = SAME.get(engine, 0.0) if source == engine else BEHIND_TENSOR if source == "tensor" else CROSS
-                start = max(start, end + lag)
-            if best is None or start < best[0]:
-                best = (start, name, engine)
-        if best is None:
-            break
-        start, name, engine = best
-        cost, needs, gives, write = streams[name][heads[name]]
+            start = free.get(engine, 0.0)
+            for maker, time in [given[x] for x in needs]:
+                start = max(start, time + (REACH[maker] if maker != engine or engine == "vector" else 0.0))
+            if first is None or start < first[0]:
+                first = (start, name, engine)
+        assert first is not None, "no stream can go on"
+        start, name, engine = first
+        length, needs, result, write = streams[name][position[name]]
         write()
-        heads[name] += 1
-        clock[engine] = start + cost
-        ready[gives] = (engine, start + cost)
-    assert all(heads[name] == len(streams[name]) for name in streams)
+        position[name] += 1
+        free[engine] = start + length
+        given[result] = (engine, start + length)
 
 
 def tile_learnedstencilwenostep_t_kernel(tc, x_bytes, x_scale, cs, ss, gamma, g, dv, out):
@@ -88,10 +81,12 @@ def tile_learnedstencilwenostep_t_kernel(tc, x_bytes, x_scale, cs, ss, gamma, g,
         psum = ctx.enter_context(tc.psum_pool(name="psum", bufs=1))
         ctx.enter_context(tc.manual_schedule())
 
-        streams = {name: [] for name in ("vector", "scalar", "gpsimd", "tensor:scalar", "tensor:vector", "sync")}
+        streams = {
+            name: [] for name in ("vector", "scalar", "gpsimd", "tensor:for_scalar", "tensor:for_vector", "sync")
+        }
 
-        def add(stream, cost, needs, gives, write):
-            streams[stream].append((cost, needs, gives, write))
+        def add(stream, length, needs, result, write):
+            streams[stream].append((length, needs, result, write))
 
         scale = keep.tile([P, 2 * D], F32, name="scale")
         scale_col = keep.tile([P, WORD], F32, name="scale_col")
@@ -103,54 +98,51 @@ def tile_learnedstencilwenostep_t_kernel(tc, x_bytes, x_scale, cs, ss, gamma, g,
         g_half = keep.tile([P, WORD], F32, name="g_half")
         ident = keep.tile([P, P], F32, name="ident")
         half = keep.tile([P, 1], F32, name="half")
-        table = keep.tile([P, 1], F32, name="table")
+        warm = keep.tile([P, 1], F32, name="warm")
         make_identity(nc, ident[:])
         nc.vector.memset(half[:], 0.5)
-        nc.scalar.activation(out=table[:], in_=half[:], func=ACT.Ln)
+        nc.scalar.activation(out=warm[:], in_=half[:], func=ACT.Ln)
 
-        codes = {}
-        scales = {}
+        codes, scales = {}, {}
         for w in ("s0", "s1", "c0", "c1", "n0", "dv"):
             codes[w] = keep.tile([P, F], U32, name="codes_" + w, align_bytes=64)
             scales[w] = keep.tile([P, F], U8, name="scales_" + w, align_bytes=64)
-        x_codes = {}
-        x_scales = {}
+        x_codes, x_scales = {}, {}
         for i in range(TILES):
             x_codes[i] = keep.tile([P, TOK], U32, name="x_codes_%d" % i, align_bytes=64)
             x_scales[i] = keep.tile([P, TOK], U8, name="x_scales_%d" % i, align_bytes=64)
 
         held = {}
 
-        def part(t):
-            return slice(t * TOK, (t + 1) * TOK)
+        def columns(part, width):
+            return slice(part * width, (part + 1) * width)
 
+        booked = {kind: 0 for kind in BANKS}
 
-        def take(name, depth, needs_of, key, shape):
-            n = used.get(name, 0)
-            used[name] = n + 1
+        def book(kind, key, shape):
+            n = booked[kind]
+            booked[kind] += 1
 
             def make():
-                held[key] = psum.tile(shape, F32, name=name, bufs=depth)
+                held[key] = psum.tile(shape, F32, name=kind, bufs=BANKS[kind])
                 return held[key]
 
-            return n, [(needs_of, n - depth)] if n >= depth else [], make
-
-        used = {}
+            return (kind, n), [(kind, n - BANKS[kind])] if n >= BANKS[kind] else [], make
 
         def load_x(i):
             def write():
-                held["bytes", i] = ring.tile([P, SUB, D], U8, name="x_raw", bufs=4)
+                held["bytes", i] = ring.tile([P, SUB, D], U8, name="bytes", bufs=4)
                 rows = x_bytes[i * TOK : (i + 1) * TOK, :]
                 nc.sync.dma_start(out=held["bytes", i][:], in_=rows.rearrange("(p b) k -> p b k", b=SUB))
 
-            add("sync", 0.5, [("wide", i - 4, 1)] if i >= 4 else [], ("bytes", i), write)
+            add("sync", 1.0, [("wide", i - 4, 1)] if i >= 4 else [], ("bytes", i), write)
 
-        def load_weight(w, source, reader):
+        def load_weight(w, source, needs):
             def write():
-                held["raw", w] = ring.tile([P, WORD, F], BF16, name="w_raw", bufs=3)
+                held["raw", w] = ring.tile([P, WORD, F], BF16, name="raw", bufs=3)
                 nc.sync.dma_start(out=held["raw", w][:], in_=source.rearrange("(p j) c -> p j c", j=WORD))
 
-            add("sync", 1.0, [("grouped", reader)] if reader else [], ("raw", w), write)
+            add("sync", 2.0, needs, ("raw", w), write)
 
         def load_scale():
             nc.sync.dma_start(out=scale_col[:], in_=x_scale.rearrange("o (p t) -> p (o t)", t=WORD))
@@ -160,36 +152,42 @@ def tile_learnedstencilwenostep_t_kernel(tc, x_bytes, x_scale, cs, ss, gamma, g,
             nc.sync.dma_start(out=g_col[:], in_=g.rearrange("(p t) -> p t", t=WORD))
 
         def spread_scale():
-            n, needs, make = take("s_bank", S_BANKS, "s_read", "spread", [P, WORD, P])
+            emptied, needs, make = book("for_scalar", "spread", [P, WORD, P])
 
-            def turn():
+            def turn_columns():
                 bank = make()
                 for t in range(WORD):
                     nc.tensor.transpose(bank[:, t, :], scale_col[:, t : t + 1].to_broadcast([P, P]), ident[:])
 
             def copy():
-                bank = held["spread"]
-                nc.scalar.copy(out=scale[:, :D].rearrange("p (n t) -> p n t", t=WORD), in_=bank[:].rearrange("p t n -> p n t"))
+                dst = scale[:, :D].rearrange("p (n t) -> p n t", t=WORD)
+                nc.scalar.copy(out=dst, in_=held["spread"][:].rearrange("p t n -> p n t"))
 
             def double():
                 nc.vector.tensor_copy(out=scale[:, D:], in_=scale[:, :D])
 
-            add("tensor:scalar", 0.5, needs + [("scale_col",)], ("spread",), turn)
-            add("scalar", 0.45, [("spread",)], ("s_read", n), copy)
-            return double
+            add("tensor:for_scalar", 1.0, needs + [("scale_col",)], ("spread",), turn_columns)
+            add("scalar", 1.0, [("spread",)], emptied, copy)
+            return emptied, double
 
         def log_gammas():
-            nc.scalar.activation(out=ln_gamma[:], in_=gamma_col[:], func=ACT.Ln)
+            def write():
+                nc.scalar.activation(out=ln_gamma[:], in_=gamma_col[:], func=ACT.Ln)
+
+            add("scalar", 0.1, [("gain_cols",)], ("ln_gamma",), write)
 
         def gains():
-            nc.vector.tensor_tensor(out=ln_ratio[:], in0=ln_gamma[:, 1, :], in1=ln_gamma[:, 0, :], op=ALU.subtract)
-            nc.vector.tensor_copy(out=g_full[:], in_=g_col[:])
-            nc.vector.tensor_scalar(out=g_half[:], in0=g_col[:], scalar1=0.5, scalar2=None, op0=ALU.mult)
+            def write():
+                nc.vector.tensor_tensor(out=ln_ratio[:], in0=ln_gamma[:, 1, :], in1=ln_gamma[:, 0, :], op=ALU.subtract)
+                nc.vector.tensor_copy(out=g_full[:], in_=g_col[:])
+                nc.vector.tensor_scalar(out=g_half[:], in0=g_col[:], scalar1=0.5, scalar2=None, op0=ALU.mult)
+
+            add("vector", 0.3, [("ln_gamma",)], ("gains",), write)
 
         def group_weight(w, engine):
             def write():
-                grouped = ring.tile([P, WORD * F], BF16, name="w_grouped", bufs=3, align_bytes=64)
-                held["grouped", w] = grouped
+                held["grouped", w] = ring.tile([P, F * WORD], BF16, name="grouped", bufs=3, align_bytes=64)
+                grouped = held["grouped", w]
                 if w == "n0":
                     nc.vector.tensor_scalar(
                         out=grouped[:], in0=held["grouped", "c0"][:], scalar1=-1.0, scalar2=None, op0=ALU.mult
@@ -207,19 +205,19 @@ def tile_learnedstencilwenostep_t_kernel(tc, x_bytes, x_scale, cs, ss, gamma, g,
                 else:
                     nc.scalar.copy(out=dst, in_=src)
 
-            cost = 0.46 if w == "n0" else 1.07 if engine == "vector" else 2.0
-            add(engine, cost, [("grouped", "c0") if w == "n0" else ("raw", w)], ("grouped", w), write)
+            length = 1.0 if w == "n0" else 2.4 if engine == "vector" else 4.4
+            add(engine, length, [("grouped", "c0") if w == "n0" else ("raw", w)], ("grouped", w), write)
 
         def quantise_weight(w):
             def write():
                 nc.vector.quantize_mx(out=codes[w][:].bitcast(FP8X4), scales=scales[w][:], in_=held["grouped", w][:])
 
-            add("vector", 0.48, [("grouped", w)], ("weight", w), write)
+            add("vector", 1.0, [("grouped", w)], ("weight", w), write)
 
-        def widen(i, h, width):
+        def widen(i, h, width, scale_ready):
             def write():
                 if h == 0:
-                    held["wide", i] = ring.tile([P, SUB * D], BF16, name="x_wide", bufs=2)
+                    held["wide", i] = ring.tile([P, SUB * D], BF16, name="wide", bufs=2)
                 src = held["bytes", i][:].rearrange("p b k -> p (b k)")
                 for c in range(2 * D * h, 2 * D * (h + 1), width):
                     nc.vector.tensor_tensor(
@@ -229,23 +227,23 @@ def tile_learnedstencilwenostep_t_kernel(tc, x_bytes, x_scale, cs, ss, gamma, g,
                         op=ALU.mult,
                     )
 
-            needs = [("bytes", i), ("s_read", 0) if width == D else ("scale",)]
-            add("vector", 0.9, needs + ([("turned", i - 2, 1)] if i >= 2 else []), ("wide", i, h), write)
+            needs = [("bytes", i), scale_ready] + ([("turned", i - 2, 1)] if i >= 2 else [])
+            add("vector", 2.0, needs, ("wide", i, h), write)
 
         def turn(i, h, reader):
-            n, needs, make = take("x_bank", X_BANKS, "x_read", ("turned", i, h), [P, 2, 2, P])
+            emptied, needs, make = book("for_" + reader, ("turned", i, h), [P, 2, 2, P])
 
             def turn_words():
                 bank = make()
                 for b in range(2):
-                    words = held["wide", i][:, (2 * h + b) * D : (2 * h + b + 1) * D].bitcast(F32)
+                    words = held["wide", i][:, columns(2 * h + b, D)].bitcast(F32)
                     for u in range(2):
                         nc.tensor.transpose(bank[:, b, u, :], words[:, u : D // 2 : 2], ident[:])
 
             def empty():
                 if h == 0:
                     held["x_grouped", i] = ring.tile([P, TOK * WORD], BF16, name="x_grouped", bufs=2, align_bytes=64)
-                dst = held["x_grouped", i][:, 1024 * h : 1024 * (h + 1)].bitcast(F32)
+                dst = held["x_grouped", i][:, columns(h, 2 * P * WORD)].bitcast(F32)
                 dst = dst.rearrange("p (b n u) -> p b n u", b=2, u=2)
                 src = held["turned", i, h][:].rearrange("p b u n -> p b n u")
                 if reader == "scalar":
@@ -253,23 +251,23 @@ def tile_learnedstencilwenostep_t_kernel(tc, x_bytes, x_scale, cs, ss, gamma, g,
                 else:
                     nc.vector.tensor_copy(out=dst, in_=src)
 
-            add("tensor:vector", 0.45, needs + [("wide", i, h)], ("turned", i, h), turn_words)
-            add(reader, 0.455, [("turned", i, h)] + ([("x", i - 2)] if i >= 2 else []), ("x_read", n), empty)
-            return n
+            add("tensor:for_" + reader, 1.0, needs + [("wide", i, h)], ("turned", i, h), turn_words)
+            add(reader, 1.0, [("turned", i, h)] + ([("x", i - 2)] if i >= 2 else []), emptied, empty)
+            return emptied
 
-        def quantise_x(i, banks):
+        def quantise_x(i, emptied):
             def write():
                 nc.vector.quantize_mx(
                     out=x_codes[i][:].bitcast(FP8X4), scales=x_scales[i][:], in_=held["x_grouped", i][:]
                 )
 
-            add("vector", 0.48, [("x_read", n) for n in banks], ("x", i), write)
+            add("vector", 1.0, emptied, ("x", i), write)
 
         def stage1(bank, w, t, i, start, stop):
             nc.tensor.matmul_mx(
                 out=bank[:],
-                lhsT=codes[w][:, P * t : P * (t + 1)].bitcast(FP8X4),
-                lhsT_scale=scales[w][:, P * t : P * (t + 1)],
+                lhsT=codes[w][:, columns(t, P)].bitcast(FP8X4),
+                lhsT_scale=scales[w][:, columns(t, P)],
                 rhs=x_codes[i][:].bitcast(FP8X4),
                 rhs_scale=x_scales[i][:],
                 start=start,
@@ -277,117 +275,124 @@ def tile_learnedstencilwenostep_t_kernel(tc, x_bytes, x_scale, cs, ss, gamma, g,
             )
 
         def square(i, k, t):
-            n, needs, make = take("s_bank", S_BANKS, "s_read", ("s_bank", i, k, t), [P, TOK])
+            emptied, needs, make = book("for_scalar", ("s_bank", i, k, t), [P, TOK])
 
             def multiply():
                 stage1(make(), "s%d" % k, t, i, True, True)
 
             def write():
                 if t == 0:
-                    held["s", i, k] = ring.tile([P, WORD * TOK], F32, name="s%d" % k, bufs=KEPT if k == 0 else 2)
-                bank = held["s_bank", i, k, t]
-                nc.scalar.activation(out=held["s", i, k][:, part(t)], in_=bank[:], func=ACT.Square)
-
-            free = []
-            if t == 0 and k == 0 and i >= KEPT:
-                free = [("d_read", WORD * (i - KEPT) + WORD - 1)]
-            if t == 0 and k == 1 and i >= 2:
-                free = [("z", i - 2)]
-            add("tensor:scalar", 0.225, needs + [("x", i), ("weight", "s%d" % k)], ("s_bank", n), multiply)
-            add("scalar", 0.45, [("s_bank", n)] + free, ("s_read", n), write)
-
-        def table_load(func):
-            change = 0.0 if current[0] == func else 1.3
-            current[0] = func
-            return change
-
-        current = [ACT.Ln]
-
-        def logarithm(i, k):
-            def write():
-                s = held["s", i, k]
-                nc.scalar.activation(out=s[:], in_=s[:], func=ACT.Ln, bias=half[:, 0:1])
-
-            add("scalar", 1.73 + table_load(ACT.Ln), [], ("ln", i, k), write)
-
-        def difference(i):
-            def write():
-                nc.vector.tensor_tensor(
-                    out=held["s", i, 0][:], in0=held["s", i, 0][:], in1=held["s", i, 1][:], op=ALU.subtract
+                    held["s", i, k] = ring.tile([P, WORD * TOK], F32, name="s%d" % k, bufs=HELD if k == 0 else 3)
+                nc.scalar.activation(
+                    out=held["s", i, k][:, columns(t, TOK)], in_=held["s_bank", i, k, t][:], func=ACT.Square
                 )
 
-            add("vector", 1.73, [("ln", i, 1)], ("z", i), write)
+            free = []
+            if t == 0 and k == 0 and i >= HELD:
+                free = [("difference", WORD * (i - HELD) + WORD - 1)]
+            if t == 0 and k == 1 and i >= 3:
+                free = [("z", i - 3, 1)]
+            add("tensor:for_scalar", MATMUL, needs + [("x", i), ("weight", "s%d" % k)], ("s_bank", i, k, t), multiply)
+            add("scalar", 1.0, [("s_bank", i, k, t)] + free, emptied, write)
+
+        table = [ACT.Ln]
+
+        def table_change(func):
+            length = 0.0 if table[0] == func else TABLE
+            table[0] = func
+            return length
+
+        def logarithm(i, h, k):
+            def write():
+                s = held["s", i, k][:, columns(h, 2 * TOK)]
+                nc.scalar.activation(out=s, in_=s, func=ACT.Ln, bias=half[:, 0:1])
+
+            add("scalar", 2.0 + table_change(ACT.Ln), [], ("ln", i, h, k), write)
+
+        def difference(i, h):
+            def write():
+                ln_0 = held["s", i, 0][:, columns(h, 2 * TOK)]
+                ln_1 = held["s", i, 1][:, columns(h, 2 * TOK)]
+                nc.vector.tensor_tensor(out=ln_0, in0=ln_0, in1=ln_1, op=ALU.subtract)
+
+            add("vector", 2.0, [("ln", i, h, 0), ("ln", i, h, 1)], ("z", i, h), write)
 
         def sigmoid(i):
             for t in range(WORD):
 
                 def write(t=t):
-                    z = held["s", i, 0][:, part(t)]
+                    z = held["s", i, 0][:, columns(t, TOK)]
                     nc.scalar.activation(out=z, in_=z, func=ACT.Sigmoid, bias=ln_ratio[:, t : t + 1], scale=2.0)
 
-                add("scalar", 0.45 + table_load(ACT.Sigmoid), [("z", i), ("gains",)], ("weighted", i, t), write)
+                add("scalar", 1.0 + table_change(ACT.Sigmoid), [("z", i, t // 2), ("gains",)], ("sigmoid", i, t), write)
 
         def blend_m(i, t):
-            n, needs, make = take("d_bank", D_BANKS, "d_read", ("d_bank", i, t), [P, TOK])
-            nq, needs_q, make_q = take("q_bank", Q_BANKS, "q_read", ("q_bank", i, t), [P, TOK])
+            emptied, needs, make = book("difference", ("d_bank", i, t), [P, TOK])
 
-            def multiply_d():
+            def multiply():
                 bank = make()
                 stage1(bank, "c1", t, i, True, False)
                 stage1(bank, "n0", t, i, False, True)
 
-            def multiply_q():
-                stage1(make_q(), "c0", t, i, True, True)
-
             def write():
                 if t == 0:
                     held["q", i] = ring.tile([P, WORD * TOK], F32, name="q", bufs=2)
-                bank = held["d_bank", i, t]
+                cols = columns(t, TOK)
                 nc.vector.tensor_tensor(
-                    out=held["q", i][:, part(t)], in0=held["s", i, 0][:, part(t)], in1=bank[:], op=ALU.mult
+                    out=held["q", i][:, cols], in0=held["s", i, 0][:, cols], in1=held["d_bank", i, t][:], op=ALU.mult
                 )
 
-            weights = [("weight", "c1"), ("weight", "n0")]
-            add("tensor:vector", 0.45, needs + weights + [("x", i)], ("d_bank", n), multiply_d)
-            add("tensor:vector", 0.225, needs_q + [("weight", "c0"), ("x", i)], ("q_bank", nq), multiply_q)
-            add("vector", 0.455, [("d_bank", n), ("weighted", i, t)], ("d_read", n), write)
-            return nq
+            needs = needs + [("weight", "c1"), ("weight", "n0"), ("x", i)]
+            add("tensor:for_vector", 2 * MATMUL, needs, ("d_bank", i, t), multiply)
+            add("vector", 1.0, [("d_bank", i, t), ("sigmoid", i, t)], emptied, write)
 
-        def blend_q(i, t, nq):
-            def write():
-                q = held["q", i][:, part(t)]
-                bank = held["q_bank", i, t]
-                nc.vector.tensor_tensor(out=q, in0=q, in1=bank[:], op=ALU.add)
+        def book_q0(i, t):
+            emptied, needs, make = book("q0", ("q_bank", i, t), [P, TOK])
+
+            def multiply():
+                stage1(make(), "c0", t, i, True, True)
+
+            def add_q0():
+                q = held["q", i][:, columns(t, TOK)]
+                nc.vector.tensor_tensor(out=q, in0=q, in1=held["q_bank", i, t][:], op=ALU.add)
+
+            engine = "vector" if i == TILES - 1 and t >= WORD // 2 else "gpsimd"
 
             def gain():
                 if t == 0:
                     held["gain", i] = ring.tile([P, WORD * TOK], F32, name="gain", bufs=2)
-                nc.gpsimd.tensor_scalar(
-                    out=held["gain", i][:, part(t)],
-                    in0=held["q", i][:, part(t)],
+                cols = columns(t, TOK)
+                (nc.vector if engine == "vector" else nc.gpsimd).tensor_scalar(
+                    out=held["gain", i][:, cols],
+                    in0=held["q", i][:, cols],
                     scalar1=g_half[:, t : t + 1],
                     scalar2=g_full[:, t : t + 1],
                     op0=ALU.mult,
                     op1=ALU.add,
                 )
 
-            add("vector", 0.455, [("q_bank", nq)], ("q_read", nq), write)
-            free = [("pg", i - 2, 1)] if i >= 2 else []
-            add("gpsimd", 0.55, [("q_read", nq), ("gains",)] + free, ("gain", i, t), gain)
+            def product():
+                add("tensor:for_vector", MATMUL, needs + [("weight", "c0"), ("x", i)], ("q_bank", i, t), multiply)
+
+            def blend_q():
+                add("vector", 1.0, [("q_bank", i, t)], emptied, add_q0)
+
+            def scale_q():
+                free = [("pg", i - 2, 1)] if i >= 2 else []
+                add(engine, 1.2, [emptied, ("gains",)] + free, ("gain", i, t), gain)
+
+            return product, blend_q, scale_q
 
         def flux(i, h):
             def write():
                 if h == 0:
                     held["pg", i] = ring.tile([P, TOK * WORD], BF16, name="pg", bufs=2, align_bytes=64)
-                dst = held["pg", i][:, 1024 * h : 1024 * (h + 1)]
-                q, gain = (
-                    held[name, i][:].rearrange("p (t h c r) -> p h c t r", t=WORD, h=2, r=RUN)[:, h] for name in ("q", "gain")
-                )
-                nc.vector.tensor_tensor(
-                    out=dst.rearrange("p (c r t) -> p c t r", r=RUN, t=WORD), in0=q, in1=gain, op=ALU.mult
-                )
+                dst = held["pg", i][:, columns(h, 2 * P * WORD)].rearrange("p (c r t) -> p c t r", r=RUN, t=WORD)
+                q = held["q", i][:].rearrange("p (t h c r) -> p h c t r", t=WORD, h=2, r=RUN)[:, h]
+                gain = held["gain", i][:].rearrange("p (t h c r) -> p h c t r", t=WORD, h=2, r=RUN)[:, h]
+                nc.vector.tensor_tensor(out=dst, in0=q, in1=gain, op=ALU.mult)
 
-            add("vector", 0.88, [("gain", i, t) for t in range(WORD)], ("pg", i, h), write)
+            add("vector", 2.0, [("gain", i, t) for t in range(WORD)], ("pg", i, h), write)
 
         def quantise_pg(i, h):
             def write():
@@ -395,153 +400,175 @@ def tile_learnedstencilwenostep_t_kernel(tc, x_bytes, x_scale, cs, ss, gamma, g,
                     held["pg_codes", i] = ring.tile([P, TOK], U32, name="pg_codes", bufs=2, align_bytes=64)
                     held["pg_scales", i] = ring.tile([P, TOK], U8, name="pg_scales", bufs=2, align_bytes=64)
                     held["out", i] = ring.tile([P, SUB, D], F32, name="out_tile", bufs=2)
-                cols = slice(256 * h, 256 * (h + 1))
                 nc.vector.quantize_mx(
-                    out=held["pg_codes", i][:, cols].bitcast(FP8X4),
-                    scales=held["pg_scales", i][:, cols],
-                    in_=held["pg", i][:, 1024 * h : 1024 * (h + 1)],
+                    out=held["pg_codes", i][:, columns(h, 2 * P)].bitcast(FP8X4),
+                    scales=held["pg_scales", i][:, columns(h, 2 * P)],
+                    in_=held["pg", i][:, columns(h, 2 * P * WORD)],
                 )
 
-            free = [("product", i - 2, SUB - 1), ("stored", i - 2)] if i >= 2 else []
-            add("vector", 0.26, [("pg", i, h)] + free, ("pg_quantised", i, h), write)
+            free = [("product", i - 2, b) for b in range(SUB)] + [("stored", i - 2)] if i >= 2 else []
+            add("vector", 0.6, [("pg", i, h)] + free, ("pg_quantised", i, h), write)
 
-        def divergence(i, b):
-            reader = "scalar" if b < OUT_ON_SCALAR else "vector"
-            name, depth = ("s", S_BANKS) if reader == "scalar" else ("x", X_BANKS)
-            n, needs, make = take(name + "_bank", depth, name + "_read", ("product", i, b), [P, D])
+        copied = {}
+
+        def divergence(i, b, reader):
+            emptied, needs, make = book("for_" + reader, ("product", i, b), [P, D])
 
             def multiply():
-                bank = make()
                 nc.tensor.matmul_mx(
-                    out=bank[:],
-                    lhsT=held["pg_codes", i][:, P * b : P * (b + 1)].bitcast(FP8X4),
-                    lhsT_scale=held["pg_scales", i][:, P * b : P * (b + 1)],
+                    out=make()[:],
+                    lhsT=held["pg_codes", i][:, columns(b, P)].bitcast(FP8X4),
+                    lhsT_scale=held["pg_scales", i][:, columns(b, P)],
                     rhs=codes["dv"][:].bitcast(FP8X4),
                     rhs_scale=scales["dv"][:],
                     start=True,
                     stop=True,
                 )
 
-            def empty():
-                dst = held["out", i][:, b, :]
-                bank = held["product", i, b]
+            def copy():
                 if reader == "scalar":
-                    nc.scalar.copy(out=dst, in_=bank[:])
+                    nc.scalar.copy(out=held["out", i][:, b, :], in_=held["product", i, b][:])
                 else:
-                    nc.vector.tensor_copy(out=dst, in_=bank[:])
+                    nc.vector.tensor_copy(out=held["out", i][:, b, :], in_=held["product", i, b][:])
 
             rows = out[i * TOK : (i + 1) * TOK, :].rearrange("(p b) d -> p b d", b=SUB)
 
             def store():
                 nc.sync.dma_start(out=rows, in_=held["out", i][:])
 
-            def store_part():
+            def store_sub_tile():
                 nc.sync.dma_start(out=rows[:, b, :], in_=held["out", i][:, b, :])
 
-            add("tensor:" + reader, 0.225, needs + [("pg_quantised", i, b // 2), ("weight", "dv")], ("product", i, b), multiply)
-            add(reader, 0.45, [("product", i, b)], (name + "_read", n), empty)
-            copied[i, b] = (name + "_read", n)
+            needs = needs + [("pg_quantised", i, b // 2), ("weight", "dv")]
+            add("tensor:for_" + reader, MATMUL, needs, ("product", i, b), multiply)
+            add(reader, 1.0, [("product", i, b)], emptied, copy)
+            copied[i, b] = emptied
             if i == TILES - 1:
-                add("sync", 0.1, [copied[i, b]], ("stored", i, b), store_part)
-            elif b == SUB - 1:
-                add("sync", 0.1, [copied[i, x] for x in range(SUB)], ("stored", i), store)
+                add("sync", 0.2, [emptied], ("stored", i, b), store_sub_tile)
+            elif all((i, x) in copied for x in range(SUB)):
+                add("sync", 0.2, [copied[i, x] for x in range(SUB)], ("stored", i), store)
 
-        copied = {}
-
-        add("sync", 0.1, [], ("scale_col",), load_scale)
+        add("sync", 0.2, [], ("scale_col",), load_scale)
         load_x(0)
-        load_weight("s1", ss[1], None)
-        load_weight("s0", ss[0], None)
+        load_weight("s1", ss[1], [])
+        load_weight("s0", ss[0], [])
         load_x(1)
-        load_weight("c1", cs[1], None)
-        add("sync", 0.1, [], ("gain_cols",), load_gains)
-        load_weight("c0", cs[0], "s1")
+        load_weight("c1", cs[1], [])
+        add("sync", 0.2, [], ("gain_cols",), load_gains)
+        load_weight("c0", cs[0], [("grouped", "s1")])
         load_x(2)
-        load_weight("dv", dv, "s0")
+        load_weight("dv", dv, [("grouped", "s0")])
         load_x(3)
-        double_scale = spread_scale()
+        scale_once, double_scale = spread_scale()
+        scale_twice = ("scale_twice",)
         group_weight("s1", "scalar")
-        widen(0, 0, D)
-        widen(0, 1, D)
+        for h in range(2):
+            widen(0, h, D, scale_once)
         group_weight("s0", "vector")
-        banks = [turn(0, h, "scalar") for h in range(2)]
+        emptied_0 = [turn(0, h, "scalar") for h in range(2)]
         quantise_weight("s1")
         quantise_weight("s0")
-        quantise_x(0, banks)
-        add("vector", 0.25, [("s_read", 0)], ("scale",), double_scale)
-        widen(1, 0, 2 * D)
-        widen(1, 1, 2 * D)
+        quantise_x(0, emptied_0)
+        add("vector", 0.6, [scale_once], scale_twice, double_scale)
+        for h in range(2):
+            widen(1, h, 2 * D, scale_twice)
+
+        later = {name: {} for name in ("logarithm", "difference", "blend_q", "flux", "quantise_pg", "divergence")}
+        now = [0]
+
+        def put(name, half_steps, *entry):
+            later[name].setdefault(now[0] + half_steps, []).append(entry)
+
+        def due(name):
+            return later[name].pop(now[0], [])
 
         pieces = []
         for w in ("c1", "c0", "n0", "dv"):
-            pieces.append((group_weight, (w, "vector")))
-            pieces.append((quantise_weight, (w,)))
+            pieces.append([(group_weight, (w, "vector"))])
+            pieces.append([(quantise_weight, (w,))])
+        pieces[3].append((log_gammas, ()))
+        pieces[5].append((gains, ()))
+        to_widen = [(i, h) for i in range(2, TILES) for h in range(2)]
+        to_turn = [(i, h) for i in range(1, TILES) for h in range(2)]
+        emptied_x = {}
 
-        last_s = None
-        last_c = None
-        for i, c, sigmoids in STEPS:
-            n = i + 1 if i is not None and i + 1 < TILES else None
-            wider = n + 1 if n is not None and n + 1 < TILES else None
-            if last_s is not None:
-                logarithm(last_s, 0)
-                logarithm(last_s, 1)
-            for x in sigmoids:
-                if x != last_s:
-                    sigmoid(x)
-
-            banks = []
+        def half_step(i, c, prepare, h):
+            gains_due = []
+            for q_tile, t, blend_q, scale_q in due("blend_q"):
+                blend_q()
+                gains_due.append(scale_q)
+                if t == WORD - 1:
+                    put("flux", 0, q_tile, 0)
+                    put("flux", 0 if q_tile == TILES - 1 else 1, q_tile, 1)
+            products = []
             if c is not None:
-                q_banks = [blend_m(c, 0), blend_m(c, 1)]
-                blend_q(c, 0, q_banks[0])
-                q_banks.append(blend_m(c, 2))
-                if n is not None:
-                    banks.append(turn(n, 0, "vector"))
-                blend_q(c, 1, q_banks[1])
-                q_banks.append(blend_m(c, 3))
-                blend_q(c, 2, q_banks[2])
-                blend_q(c, 3, q_banks[3])
-                if n is not None:
-                    banks.append(turn(n, 1, "vector"))
-            elif n is not None:
-                for h in range(2):
-                    banks.append(turn(n, h, "vector"))
-                    if wider is not None:
-                        widen(wider, h, 2 * D)
-            if last_s is not None:
-                difference(last_s)
-            if last_s in sigmoids:
-                sigmoid(last_s)
-
-            if i == GAINS_STEP:
-                add("scalar", 0.05, [("gain_cols",)], ("ln_gamma",), log_gammas)
-                add("vector", 0.15, [("ln_gamma",)], ("gains",), gains)
-
-            for t in range(WORD):
+                for t in (2 * h, 2 * h + 1):
+                    blend_m(c, t)
+                    product, blend_q, scale_q = book_q0(c, t)
+                    products.append(product)
+                    put("blend_q", 1, c, t, blend_q, scale_q)
+            turned = None
+            if prepare and to_turn:
+                turned = to_turn.pop(0)
+                emptied_x[turned] = turn(turned[0], turned[1], "vector")
+            for call in products + gains_due:
+                call()
+            if prepare and to_widen:
+                tile, part = to_widen.pop(0)
+                widen(tile, part, 2 * D, scale_twice)
+            for entry in due("quantise_pg"):
+                quantise_pg(*entry)
+                for b in (2 * entry[1], 2 * entry[1] + 1):
+                    put("divergence", 1, entry[0], b)
+            for entry in due("flux"):
+                flux(*entry)
+                put("quantise_pg", 1, *entry)
+            out_due = due("divergence")
+            on_vector = [e for e in out_due if e[0] < OUT_ON_VECTOR and e[1] > 0]
+            on_scalar = [e for e in out_due if e not in on_vector]
+            for entry in on_vector:
+                divergence(entry[0], entry[1], "vector")
+            for entry in due("difference"):
+                difference(*entry)
+            if pieces:
+                for prepare_weight, args in pieces.pop(0):
+                    prepare_weight(*args)
+            if turned is not None and turned[1] == 1:
+                quantise_x(turned[0], [emptied_x[turned[0], 0], emptied_x[turned]])
+            logs_due = due("logarithm")
+            for k in range(2):
                 if i is not None:
-                    square(i, 0, t)
-                    square(i, 1, t)
-                if last_c is not None and t < OUT_ON_SCALAR:
-                    divergence(last_c, t)
-            if last_c is not None:
-                for b in range(OUT_ON_SCALAR, SUB):
-                    divergence(last_c, b)
-            if n is not None:
-                quantise_x(n, banks)
+                    square(i, 0, 2 * h + k)
+                    square(i, 1, 2 * h + k)
+                for entry in logs_due:
+                    logarithm(entry[0], entry[1], k)
+                if on_scalar:
+                    entry = on_scalar.pop(0)
+                    divergence(entry[0], entry[1], "scalar")
+            for entry in on_scalar:
+                divergence(entry[0], entry[1], "scalar")
+            for entry in logs_due:
+                put("difference", 2, *entry)
+            if i is not None:
+                put("logarithm", 1, i, h)
+            now[0] += 1
+
+        for i, c, sigmoids in STEPS:
+            if sigmoids:
+                for entry in due("logarithm"):
+                    logarithm(entry[0], entry[1], 0)
+                    logarithm(entry[0], entry[1], 1)
+                    early = later["difference"].pop(now[0] + 1, [])
+                    later["difference"].setdefault(now[0], []).extend(early)
+                    put("difference", 1, *entry)
+                for x in sigmoids[:-1]:
+                    sigmoid(x)
+            for h in range(2):
+                half_step(i, c, i is not None or len(sigmoids) > 0, h)
+            if sigmoids:
+                sigmoid(sigmoids[-1])
             if i is not None and i + 4 < TILES:
                 load_x(i + 4)
-            for run, args in pieces[:PIECES]:
-                run(*args)
-            pieces = pieces[PIECES:]
-            if c is not None:
-                flux(c, 0)
-                flux(c, 1)
-                if wider is not None:
-                    widen(wider, 0, 2 * D)
-                quantise_pg(c, 0)
-                if wider is not None:
-                    widen(wider, 1, 2 * D)
-                quantise_pg(c, 1)
-            last_s, last_c = i, c
-        for b in range(SUB):
-            divergence(last_c, b)
+        while any(len(later[name]) > 0 for name in later):
+            half_step(None, None, False, 0)
         issue(streams)

from contextlib import ExitStack

import concourse.mybir as mybir
from concourse.masks import make_identity

B, D, F = 4096, 512, 512
FLOPS = 5 * 2 * B * D * F

P = 128
WORD = 4
TOK = 512
TILES = B // TOK
SUB = TOK // P

F32 = mybir.dt.float32
BF16 = mybir.dt.bfloat16
U32 = mybir.dt.uint32
U8 = mybir.dt.uint8
FP8 = mybir.dt.float8_e4m3fn
FP8X4 = mybir.dt.float8_e4m3fn_x4
ALU = mybir.AluOpType
ACT = mybir.ActivationFunctionType

STEPS = (
    (0, None, ()),
    (1, None, ()),
    (2, None, ()),
    (None, None, (0, 1, 2)),
    (3, 0, ()),
    (4, None, ()),
    (5, 1, ()),
    (None, 2, (3, 4, 5)),
    (6, 3, ()),
    (7, 4, ()),
    (None, 5, (6, 7)),
    (None, 6, ()),
    (None, 7, ()),
)
HELD = 7
BANKS = {"for_scalar": 3, "for_vector": 1, "difference": 2, "q0": 2}
OUT_ON_VECTOR = 2
RUN = 4

MATMUL = 0.5
TABLE = 3.0
REACH = {"vector": 0.5, "scalar": 0.5, "gpsimd": 0.5, "sync": 0.5, "tensor": 2.0}


def issue(streams):
    given = {}
    free = {}
    position = {name: 0 for name in streams}
    while any(position[name] < len(streams[name]) for name in streams):
        first = None
        for name in streams:
            if position[name] == len(streams[name]):
                continue
            engine = name.split(":")[0]
            needs = streams[name][position[name]][1]
            if not all(x in given for x in needs):
                continue
            start = free.get(engine, 0.0)
            for maker, time in [given[x] for x in needs]:
                start = max(start, time + (REACH[maker] if maker != engine or engine == "vector" else 0.0))
            if first is None or start < first[0]:
                first = (start, name, engine)
        assert first is not None, "no stream can go on"
        start, name, engine = first
        length, needs, result, write = streams[name][position[name]]
        write()
        position[name] += 1
        free[engine] = start + length
        given[result] = (engine, start + length)


def tile_learnedstencilwenostep_t_kernel(tc, x_bytes, x_scale, cs, ss, gamma, g, dv, out):
    nc = tc.nc
    with ExitStack() as ctx:
        keep = ctx.enter_context(tc.tile_pool(name="keep", bufs=1))
        ring = ctx.enter_context(tc.tile_pool(name="ring", bufs=2))
        psum = ctx.enter_context(tc.psum_pool(name="psum", bufs=1))
        ctx.enter_context(tc.manual_schedule())

        streams = {
            name: [] for name in ("vector", "scalar", "gpsimd", "tensor:for_scalar", "tensor:for_vector", "sync")
        }

        def add(stream, length, needs, result, write):
            streams[stream].append((length, needs, result, write))

        scale = keep.tile([P, 2 * D], F32, name="scale")
        scale_col = keep.tile([P, WORD], F32, name="scale_col")
        gamma_col = keep.tile([P, 2, WORD], BF16, name="gamma_col")
        g_col = keep.tile([P, WORD], BF16, name="g_col")
        ln_gamma = keep.tile([P, 2, WORD], F32, name="ln_gamma")
        ln_ratio = keep.tile([P, WORD], F32, name="ln_ratio")
        g_full = keep.tile([P, WORD], F32, name="g_full")
        g_half = keep.tile([P, WORD], F32, name="g_half")
        ident = keep.tile([P, P], F32, name="ident")
        half = keep.tile([P, 1], F32, name="half")
        warm = keep.tile([P, 1], F32, name="warm")
        make_identity(nc, ident[:])
        nc.vector.memset(half[:], 0.5)
        nc.scalar.activation(out=warm[:], in_=half[:], func=ACT.Ln)

        codes, scales = {}, {}
        for w in ("s0", "s1", "c0", "c1", "n0", "dv"):
            codes[w] = keep.tile([P, F], U32, name="codes_" + w, align_bytes=64)
            scales[w] = keep.tile([P, F], U8, name="scales_" + w, align_bytes=64)
        x_codes, x_scales = {}, {}
        for i in range(TILES):
            x_codes[i] = keep.tile([P, TOK], U32, name="x_codes_%d" % i, align_bytes=64)
            x_scales[i] = keep.tile([P, TOK], U8, name="x_scales_%d" % i, align_bytes=64)

        held = {}

        def columns(part, width):
            return slice(part * width, (part + 1) * width)

        booked = {kind: 0 for kind in BANKS}

        def book(kind, key, shape):
            n = booked[kind]
            booked[kind] += 1

            def make():
                held[key] = psum.tile(shape, F32, name=kind, bufs=BANKS[kind])
                return held[key]

            return (kind, n), [(kind, n - BANKS[kind])] if n >= BANKS[kind] else [], make

        def load_x(i):
            def write():
                held["bytes", i] = ring.tile([P, SUB, D], U8, name="bytes", bufs=4)
                rows = x_bytes[i * TOK : (i + 1) * TOK, :]
                nc.sync.dma_start(out=held["bytes", i][:], in_=rows.rearrange("(p b) k -> p b k", b=SUB))

            add("sync", 1.0, [("wide", i - 4, 1)] if i >= 4 else [], ("bytes", i), write)

        def load_weight(w, source, needs):
            def write():
                held["raw", w] = ring.tile([P, WORD, F], BF16, name="raw", bufs=3)
                nc.sync.dma_start(out=held["raw", w][:], in_=source.rearrange("(p j) c -> p j c", j=WORD))

            add("sync", 2.0, needs, ("raw", w), write)

        def load_scale():
            nc.sync.dma_start(out=scale_col[:], in_=x_scale.rearrange("o (p t) -> p (o t)", t=WORD))

        def load_gains():
            nc.sync.dma_start(out=gamma_col[:], in_=gamma.rearrange("k (p t) -> p k t", t=WORD))
            nc.sync.dma_start(out=g_col[:], in_=g.rearrange("(p t) -> p t", t=WORD))

        def spread_scale():
            emptied, needs, make = book("for_scalar", "spread", [P, WORD, P])

            def turn_columns():
                bank = make()
                for t in range(WORD):
                    nc.tensor.transpose(bank[:, t, :], scale_col[:, t : t + 1].to_broadcast([P, P]), ident[:])

            def copy():
                dst = scale[:, :D].rearrange("p (n t) -> p n t", t=WORD)
                nc.scalar.copy(out=dst, in_=held["spread"][:].rearrange("p t n -> p n t"))

            def double():
                nc.vector.tensor_copy(out=scale[:, D:], in_=scale[:, :D])

            add("tensor:for_scalar", 1.0, needs + [("scale_col",)], ("spread",), turn_columns)
            add("scalar", 1.0, [("spread",)], emptied, copy)
            return emptied, double

        def log_gammas():
            def write():
                nc.scalar.activation(out=ln_gamma[:], in_=gamma_col[:], func=ACT.Ln)

            add("scalar", 0.1, [("gain_cols",)], ("ln_gamma",), write)

        def gains():
            def write():
                nc.vector.tensor_tensor(out=ln_ratio[:], in0=ln_gamma[:, 1, :], in1=ln_gamma[:, 0, :], op=ALU.subtract)
                nc.vector.tensor_copy(out=g_full[:], in_=g_col[:])
                nc.vector.tensor_scalar(out=g_half[:], in0=g_col[:], scalar1=0.5, scalar2=None, op0=ALU.mult)

            add("vector", 0.3, [("ln_gamma",)], ("gains",), write)

        def group_weight(w, engine):
            def write():
                held["grouped", w] = ring.tile([P, F * WORD], BF16, name="grouped", bufs=3, align_bytes=64)
                grouped = held["grouped", w]
                if w == "n0":
                    nc.vector.tensor_scalar(
                        out=grouped[:], in0=held["grouped", "c0"][:], scalar1=-1.0, scalar2=None, op0=ALU.mult
                    )
                    return
                raw = held["raw", w]
                if w == "dv":
                    dst = grouped[:].rearrange("p (c j) -> p c j", j=WORD)
                    src = raw[:].rearrange("p j c -> p c j")
                else:
                    dst = grouped[:].rearrange("p (t m j) -> p t m j", t=WORD, j=WORD)
                    src = raw[:].rearrange("p j (m t) -> p t m j", t=WORD)
                if engine == "vector":
                    nc.vector.tensor_copy(out=dst, in_=src)
                else:
                    nc.scalar.copy(out=dst, in_=src)

            length = 1.0 if w == "n0" else 2.4 if engine == "vector" else 4.4
            add(engine, length, [("grouped", "c0") if w == "n0" else ("raw", w)], ("grouped", w), write)

        def quantise_weight(w):
            def write():
                nc.vector.quantize_mx(out=codes[w][:].bitcast(FP8X4), scales=scales[w][:], in_=held["grouped", w][:])

            add("vector", 1.0, [("grouped", w)], ("weight", w), write)

        def widen(i, h, width, scale_ready):
            def write():
                if h == 0:
                    held["wide", i] = ring.tile([P, SUB * D], BF16, name="wide", bufs=2)
                src = held["bytes", i][:].rearrange("p b k -> p (b k)")
                for c in range(2 * D * h, 2 * D * (h + 1), width):
                    nc.vector.tensor_tensor(
                        out=held["wide", i][:, c : c + width],
                        in0=src[:, c : c + width].bitcast(FP8),
                        in1=scale[:, :width],
                        op=ALU.mult,
                    )

            needs = [("bytes", i), scale_ready] + ([("turned", i - 2, 1)] if i >= 2 else [])
            add("vector", 2.0, needs, ("wide", i, h), write)

        def turn(i, h, reader):
            emptied, needs, make = book("for_" + reader, ("turned", i, h), [P, 2, 2, P])

            def turn_words():
                bank = make()
                for b in range(2):
                    words = held["wide", i][:, columns(2 * h + b, D)].bitcast(F32)
                    for u in range(2):
                        nc.tensor.transpose(bank[:, b, u, :], words[:, u : D // 2 : 2], ident[:])

            def empty():
                if h == 0:
                    held["x_grouped", i] = ring.tile([P, TOK * WORD], BF16, name="x_grouped", bufs=2, align_bytes=64)
                dst = held["x_grouped", i][:, columns(h, 2 * P * WORD)].bitcast(F32)
                dst = dst.rearrange("p (b n u) -> p b n u", b=2, u=2)
                src = held["turned", i, h][:].rearrange("p b u n -> p b n u")
                if reader == "scalar":
                    nc.scalar.copy(out=dst, in_=src)
                else:
                    nc.vector.tensor_copy(out=dst, in_=src)

            add("tensor:for_" + reader, 1.0, needs + [("wide", i, h)], ("turned", i, h), turn_words)
            add(reader, 1.0, [("turned", i, h)] + ([("x", i - 2)] if i >= 2 else []), emptied, empty)
            return emptied

        def quantise_x(i, emptied):
            def write():
                nc.vector.quantize_mx(
                    out=x_codes[i][:].bitcast(FP8X4), scales=x_scales[i][:], in_=held["x_grouped", i][:]
                )

            add("vector", 1.0, emptied, ("x", i), write)

        def stage1(bank, w, t, i, start, stop):
            nc.tensor.matmul_mx(
                out=bank[:],
                lhsT=codes[w][:, columns(t, P)].bitcast(FP8X4),
                lhsT_scale=scales[w][:, columns(t, P)],
                rhs=x_codes[i][:].bitcast(FP8X4),
                rhs_scale=x_scales[i][:],
                start=start,
                stop=stop,
            )

        def square(i, k, t):
            emptied, needs, make = book("for_scalar", ("s_bank", i, k, t), [P, TOK])

            def multiply():
                stage1(make(), "s%d" % k, t, i, True, True)

            def write():
                if t == 0:
                    held["s", i, k] = ring.tile([P, WORD * TOK], F32, name="s%d" % k, bufs=HELD if k == 0 else 3)
                nc.scalar.activation(
                    out=held["s", i, k][:, columns(t, TOK)], in_=held["s_bank", i, k, t][:], func=ACT.Square
                )

            free = []
            if t == 0 and k == 0 and i >= HELD:
                free = [("difference", WORD * (i - HELD) + WORD - 1)]
            if t == 0 and k == 1 and i >= 3:
                free = [("z", i - 3, 1)]
            add("tensor:for_scalar", MATMUL, needs + [("x", i), ("weight", "s%d" % k)], ("s_bank", i, k, t), multiply)
            add("scalar", 1.0, [("s_bank", i, k, t)] + free, emptied, write)

        table = [ACT.Ln]

        def table_change(func):
            length = 0.0 if table[0] == func else TABLE
            table[0] = func
            return length

        def logarithm(i, h, k):
            def write():
                s = held["s", i, k][:, columns(h, 2 * TOK)]
                nc.scalar.activation(out=s, in_=s, func=ACT.Ln, bias=half[:, 0:1])

            add("scalar", 2.0 + table_change(ACT.Ln), [], ("ln", i, h, k), write)

        def difference(i, h):
            def write():
                ln_0 = held["s", i, 0][:, columns(h, 2 * TOK)]
                ln_1 = held["s", i, 1][:, columns(h, 2 * TOK)]
                nc.vector.tensor_tensor(out=ln_0, in0=ln_0, in1=ln_1, op=ALU.subtract)

            add("vector", 2.0, [("ln", i, h, 0), ("ln", i, h, 1)], ("z", i, h), write)

        def sigmoid(i):
            for t in range(WORD):

                def write(t=t):
                    z = held["s", i, 0][:, columns(t, TOK)]
                    nc.scalar.activation(out=z, in_=z, func=ACT.Sigmoid, bias=ln_ratio[:, t : t + 1], scale=2.0)

                add("scalar", 1.0 + table_change(ACT.Sigmoid), [("z", i, t // 2), ("gains",)], ("sigmoid", i, t), write)

        def blend_m(i, t):
            emptied, needs, make = book("difference", ("d_bank", i, t), [P, TOK])

            def multiply():
                bank = make()
                stage1(bank, "c1", t, i, True, False)
                stage1(bank, "n0", t, i, False, True)

            def write():
                if t == 0:
                    held["q", i] = ring.tile([P, WORD * TOK], F32, name="q", bufs=2)
                cols = columns(t, TOK)
                nc.vector.tensor_tensor(
                    out=held["q", i][:, cols], in0=held["s", i, 0][:, cols], in1=held["d_bank", i, t][:], op=ALU.mult
                )

            needs = needs + [("weight", "c1"), ("weight", "n0"), ("x", i)]
            add("tensor:for_vector", 2 * MATMUL, needs, ("d_bank", i, t), multiply)
            add("vector", 1.0, [("d_bank", i, t), ("sigmoid", i, t)], emptied, write)

        def book_q0(i, t):
            emptied, needs, make = book("q0", ("q_bank", i, t), [P, TOK])

            def multiply():
                stage1(make(), "c0", t, i, True, True)

            def add_q0():
                q = held["q", i][:, columns(t, TOK)]
                nc.vector.tensor_tensor(out=q, in0=q, in1=held["q_bank", i, t][:], op=ALU.add)

            engine = "vector" if i == TILES - 1 and t >= WORD // 2 else "gpsimd"

            def gain():
                if t == 0:
                    held["gain", i] = ring.tile([P, WORD * TOK], F32, name="gain", bufs=2)
                cols = columns(t, TOK)
                (nc.vector if engine == "vector" else nc.gpsimd).tensor_scalar(
                    out=held["gain", i][:, cols],
                    in0=held["q", i][:, cols],
                    scalar1=g_half[:, t : t + 1],
                    scalar2=g_full[:, t : t + 1],
                    op0=ALU.mult,
                    op1=ALU.add,
                )

            def product():
                add("tensor:for_vector", MATMUL, needs + [("weight", "c0"), ("x", i)], ("q_bank", i, t), multiply)

            def blend_q():
                add("vector", 1.0, [("q_bank", i, t)], emptied, add_q0)

            def scale_q():
                free = [("pg", i - 2, 1)] if i >= 2 else []
                add(engine, 1.2, [emptied, ("gains",)] + free, ("gain", i, t), gain)

            return product, blend_q, scale_q

        def flux(i, h):
            def write():
                if h == 0:
                    held["pg", i] = ring.tile([P, TOK * WORD], BF16, name="pg", bufs=2, align_bytes=64)
                dst = held["pg", i][:, columns(h, 2 * P * WORD)].rearrange("p (c r t) -> p c t r", r=RUN, t=WORD)
                q = held["q", i][:].rearrange("p (t h c r) -> p h c t r", t=WORD, h=2, r=RUN)[:, h]
                gain = held["gain", i][:].rearrange("p (t h c r) -> p h c t r", t=WORD, h=2, r=RUN)[:, h]
                nc.vector.tensor_tensor(out=dst, in0=q, in1=gain, op=ALU.mult)

            add("vector", 2.0, [("gain", i, t) for t in range(WORD)], ("pg", i, h), write)

        def quantise_pg(i, h):
            def write():
                if h == 0:
                    held["pg_codes", i] = ring.tile([P, TOK], U32, name="pg_codes", bufs=2, align_bytes=64)
                    held["pg_scales", i] = ring.tile([P, TOK], U8, name="pg_scales", bufs=2, align_bytes=64)
                    held["out", i] = ring.tile([P, SUB, D], F32, name="out_tile", bufs=2)
                nc.vector.quantize_mx(
                    out=held["pg_codes", i][:, columns(h, 2 * P)].bitcast(FP8X4),
                    scales=held["pg_scales", i][:, columns(h, 2 * P)],
                    in_=held["pg", i][:, columns(h, 2 * P * WORD)],
                )

            free = [("product", i - 2, b) for b in range(SUB)] + [("stored", i - 2)] if i >= 2 else []
            add("vector", 0.6, [("pg", i, h)] + free, ("pg_quantised", i, h), write)

        copied = {}

        def divergence(i, b, reader):
            emptied, needs, make = book("for_" + reader, ("product", i, b), [P, D])

            def multiply():
                nc.tensor.matmul_mx(
                    out=make()[:],
                    lhsT=held["pg_codes", i][:, columns(b, P)].bitcast(FP8X4),
                    lhsT_scale=held["pg_scales", i][:, columns(b, P)],
                    rhs=codes["dv"][:].bitcast(FP8X4),
                    rhs_scale=scales["dv"][:],
                    start=True,
                    stop=True,
                )

            def copy():
                if reader == "scalar":
                    nc.scalar.copy(out=held["out", i][:, b, :], in_=held["product", i, b][:])
                else:
                    nc.vector.tensor_copy(out=held["out", i][:, b, :], in_=held["product", i, b][:])

            rows = out[i * TOK : (i + 1) * TOK, :].rearrange("(p b) d -> p b d", b=SUB)

            def store():
                nc.sync.dma_start(out=rows, in_=held["out", i][:])

            def store_sub_tile():
                nc.sync.dma_start(out=rows[:, b, :], in_=held["out", i][:, b, :])

            needs = needs + [("pg_quantised", i, b // 2), ("weight", "dv")]
            add("tensor:for_" + reader, MATMUL, needs, ("product", i, b), multiply)
            add(reader, 1.0, [("product", i, b)], emptied, copy)
            copied[i, b] = emptied
            if i == TILES - 1:
                add("sync", 0.2, [emptied], ("stored", i, b), store_sub_tile)
            elif all((i, x) in copied for x in range(SUB)):
                add("sync", 0.2, [copied[i, x] for x in range(SUB)], ("stored", i), store)

        add("sync", 0.2, [], ("scale_col",), load_scale)
        load_x(0)
        load_weight("s1", ss[1], [])
        load_weight("s0", ss[0], [])
        load_x(1)
        load_weight("c1", cs[1], [])
        add("sync", 0.2, [], ("gain_cols",), load_gains)
        load_weight("c0", cs[0], [("grouped", "s1")])
        load_x(2)
        load_weight("dv", dv, [("grouped", "s0")])
        load_x(3)
        scale_once, double_scale = spread_scale()
        scale_twice = ("scale_twice",)
        group_weight("s1", "scalar")
        for h in range(2):
            widen(0, h, D, scale_once)
        group_weight("s0", "vector")
        emptied_0 = [turn(0, h, "scalar") for h in range(2)]
        quantise_weight("s1")
        quantise_weight("s0")
        quantise_x(0, emptied_0)
        add("vector", 0.6, [scale_once], scale_twice, double_scale)
        for h in range(2):
            widen(1, h, 2 * D, scale_twice)

        later = {name: {} for name in ("logarithm", "difference", "blend_q", "flux", "quantise_pg", "divergence")}
        now = [0]

        def put(name, half_steps, *entry):
            later[name].setdefault(now[0] + half_steps, []).append(entry)

        def due(name):
            return later[name].pop(now[0], [])

        pieces = []
        for w in ("c1", "c0", "n0", "dv"):
            pieces.append([(group_weight, (w, "vector"))])
            pieces.append([(quantise_weight, (w,))])
        pieces[3].append((log_gammas, ()))
        pieces[5].append((gains, ()))
        to_widen = [(i, h) for i in range(2, TILES) for h in range(2)]
        to_turn = [(i, h) for i in range(1, TILES) for h in range(2)]
        emptied_x = {}

        def half_step(i, c, prepare, h):
            gains_due = []
            for q_tile, t, blend_q, scale_q in due("blend_q"):
                blend_q()
                gains_due.append(scale_q)
                if t == WORD - 1:
                    put("flux", 0, q_tile, 0)
                    put("flux", 0 if q_tile == TILES - 1 else 1, q_tile, 1)
            products = []
            if c is not None:
                for t in (2 * h, 2 * h + 1):
                    blend_m(c, t)
                    product, blend_q, scale_q = book_q0(c, t)
                    products.append(product)
                    put("blend_q", 1, c, t, blend_q, scale_q)
            turned = None
            if prepare and to_turn:
                turned = to_turn.pop(0)
                emptied_x[turned] = turn(turned[0], turned[1], "vector")
            for call in products + gains_due:
                call()
            if prepare and to_widen:
                tile, part = to_widen.pop(0)
                widen(tile, part, 2 * D, scale_twice)
            for entry in due("quantise_pg"):
                quantise_pg(*entry)
                for b in (2 * entry[1], 2 * entry[1] + 1):
                    put("divergence", 1, entry[0], b)
            for entry in due("flux"):
                flux(*entry)
                put("quantise_pg", 1, *entry)
            out_due = due("divergence")
            on_vector = [e for e in out_due if e[0] < OUT_ON_VECTOR and e[1] > 0]
            on_scalar = [e for e in out_due if e not in on_vector]
            for entry in on_vector:
                divergence(entry[0], entry[1], "vector")
            for entry in due("difference"):
                difference(*entry)
            if pieces:
                for prepare_weight, args in pieces.pop(0):
                    prepare_weight(*args)
            if turned is not None and turned[1] == 1:
                quantise_x(turned[0], [emptied_x[turned[0], 0], emptied_x[turned]])
            logs_due = due("logarithm")
            for k in range(2):
                if i is not None:
                    square(i, 0, 2 * h + k)
                    square(i, 1, 2 * h + k)
                for entry in logs_due:
                    logarithm(entry[0], entry[1], k)
                if on_scalar:
                    entry = on_scalar.pop(0)
                    divergence(entry[0], entry[1], "scalar")
            for entry in on_scalar:
                divergence(entry[0], entry[1], "scalar")
            for entry in logs_due:
                put("difference", 2, *entry)
            if i is not None:
                put("logarithm", 1, i, h)
            now[0] += 1

        for i, c, sigmoids in STEPS:
            if sigmoids:
                for entry in due("logarithm"):
                    logarithm(entry[0], entry[1], 0)
                    logarithm(entry[0], entry[1], 1)
                    early = later["difference"].pop(now[0] + 1, [])
                    later["difference"].setdefault(now[0], []).extend(early)
                    put("difference", 1, *entry)
                for x in sigmoids[:-1]:
                    sigmoid(x)
            for h in range(2):
                half_step(i, c, i is not None or len(sigmoids) > 0, h)
            if sigmoids:
                sigmoid(sigmoids[-1])
            if i is not None and i + 4 < TILES:
                load_x(i + 4)
        while any(len(later[name]) > 0 for name in later):
            half_step(None, None, False, 0)
        issue(streams)
